import numpy as np, ml_dtypes
CORES = [3,11,19,27,35,43,51,59]
N = 8
BF = ml_dtypes.bfloat16
def gentries(a):
    return np.ascontiguousarray(a.reshape(8, 16, -1).transpose(0, 2, 1)).reshape(8, -1)
def gtable(e):
    e = np.asarray(e); return np.ascontiguousarray(e.reshape(8, -1, 16).transpose(0, 2, 1)).reshape(128, -1).astype(np.int32)
C, CAP, P, H = 1024, 160, 8192, 2
def walk(cells, first, pads):
    x = cells.astype(np.float32).astype(np.int32).reshape(N, 8, 16, C); p = pads.astype(np.float32).astype(np.int32).reshape(N, 8, 16, P)
    keys = [gentries(a) for a in first]; most = 0; sent = {}
    now = {(r, g): (x[r, g], keys[r][g]) for r in range(N) for g in range(8)}
    for h in range(H):
        sent = {}
        for r in range(N):
            for g in range(8):
                v, key = now[r, g]; v = (v - p[r, g][:, key]) & 255
                to = v[0] & (N - 1); key = v[1] + 256 * (v[2] & (P // 256 - 1))
                for q in range(N):
                    m = to == q; sent[r, q, g] = (v[:, m], key[m]); most = max(most, int(np.count_nonzero(m)))
        now = {(q, g): (np.concatenate([sent[r, q, g][0] for r in range(N)], axis=1), np.concatenate([sent[r, q, g][1] for r in range(N)])) for q in range(N) for g in range(8)}
    return sent, most
def parts(rng, n, w, t=-1):
    w = np.array(w, np.float64); k = 0
    if t >= 0:
        w[t] = 0; k = min(n, CAP)
    a = np.add.accumulate(w); i = np.searchsorted(a, rng.random(n - k) * a[-1], side="right")
    c = np.minimum(np.bincount(np.minimum(i, N - 1), minlength=N), CAP)
    if t >= 0: c[t] = k
    o = rng.permutation(N); o = o[np.argsort(w[o] == 0, kind="stable")]
    for r in o: c[r] += min(n - int(np.sum(c)), CAP - int(c[r]))
    return c
def routes(rng, count, runs=False):
    to = np.zeros((8, N, C, H), np.int64)
    for g in range(8):
        at = np.repeat(np.arange(N), C); t = to[g].reshape(N * C, H)
        for h in range(H):
            new = at.copy()
            for q in range(N):
                i = np.nonzero(at == q)[0]; d = np.repeat(np.arange(N), count(h, g, q, len(i)))
                new[i] = d if runs and g % 2 == 0 else rng.permutation(d)
            t[:, h] = new; at = new
    return to
def dress(to, first, p, body, u):
    x = body.copy()
    for g in range(8):
        for r in range(N):
            key = np.arange(P); at = np.full(P, r); v = np.stack([at, key & 255, key >> 8]); code = np.zeros(P, np.int64)
            for h in range(1, H):
                v = (v - np.stack([p[at, g, s, key] for s in range(3)])) & 255
                at = v[0] & (N - 1); key = v[1] + 256 * (v[2] & (P // 256 - 1)); code = code * N + at
            order = np.argsort(code, kind="stable"); a = np.searchsorted(code[order], np.arange(N ** (H - 1))); b = np.searchsorted(code[order], np.arange(N ** (H - 1)), side="right")
            q, i = np.nonzero(to[g, :, :, 0] == r); c = np.zeros(len(q), np.int64)
            for h in range(1, H): c = c * N + to[g, q, i, h]
            k = order[a[c] + np.floor(u[q, g, i] * (b - a)[c]).astype(np.int64)]
            x[q, g, 0, i] = x[q, g, 0, i] // N * N + r
            x[q, g, 1, i] = k & 255
            x[q, g, 2, i] = x[q, g, 2, i] // (P // 256) * (P // 256) + (k >> 8)
    x = (x + np.take_along_axis(p, first[:, :, None, :], axis=3)) & 255
    return {"cells": x.reshape(N, 128, C).astype(np.float32).astype(BF), "first": np.stack([gtable(e) for e in first]), "pads": p.reshape(N, 128, P).astype(np.float32).astype(BF)}
def setup_inputs(rng):
    w = 1 + rng.random((H, 8, N, N)); to = routes(rng, lambda h, g, q, n: parts(rng, n, w[h, g, q]))
    return dress(to, rng.integers(0, P, (N, 8, C)), rng.integers(0, 256, (N, 8, 16, P)), rng.integers(0, 256, (N, 8, 16, C)), rng.random((N, 8, C)))
def setup_inputs_ends(rng):
    w = 1 + rng.random((H, 8, N, N)); to = routes(rng, lambda h, g, q, n: parts(rng, n, w[h, g, q]))
    p = rng.integers(0, 256, (N, 8, 16, P)); p[0, :, :, 0] = 0
    full = rng.integers(0, 2, (N, 8, C)); body = rng.integers(0, 256, (N, 8, 16, C)) * full[:, :, None, :]
    u = rng.integers(0, 2, (N, 8, C)) * (1 - 2.0 ** -20)
    assert ((to == 0).all(axis=3).transpose(1, 0, 2) & (full == 0) & (u == 0)).any()
    return dress(to, rng.integers(0, 2, (N, 8, C)) * (P - 1), p, body, u)
def setup_inputs_full(rng):
    t = rng.integers(0, N, (H, 8)); to = routes(rng, lambda h, g, q, n: parts(rng, n, np.ones(N), int(t[h, g])), True)
    return dress(to, rng.integers(0, P, (N, 8, C)), rng.integers(0, 256, (N, 8, 16, P)), rng.integers(0, 256, (N, 8, 16, C)), rng.random((N, 8, C)))
def setup_inputs_bare(rng):
    s = rng.integers(0, N, H)
    def count(h, g, q, n):
        w = np.ones(N); none = (g % 2 == 0 and h == 0) or (g % 2 == 1 and h == H - 1)
        w[(g // 2 + s[h]) % N if none else (q + g + s[h]) % N] = 0
        return parts(rng, n, w)
    to = routes(rng, count)
    return dress(to, rng.integers(0, P, (N, 8, C)), rng.integers(0, 256, (N, 8, 16, P)), rng.integers(0, 256, (N, 8, 16, C)), rng.random((N, 8, C)))
def setup_inputs_spread(rng):
    w = np.exp2(rng.integers(-4, 5, (H, 8, N, N))); to = routes(rng, lambda h, g, q, n: parts(rng, n, w[h, g, q]))
    def skew(k):
        return np.minimum(np.floor(256 * rng.random((N, 8, 16, k)) ** np.exp2(rng.integers(-3, 4, (N, 8, 16, 1)))), 255).astype(np.int64)
    p = skew(P); p[:, :, :3] = rng.integers(0, 256, (N, 8, 3, P))
    return dress(to, rng.integers(0, P, (N, 8, C)), p, skew(C), rng.random((N, 8, C)))
def check_inputs(d):
    bad = []
    for a in ("cells", "pads"):
        v = d[a].astype(np.float32)
        if not ((v >= 0) & (v <= 255) & (v == np.floor(v))).all(): bad.append(a)
    if not ((d["first"] >= 0) & (d["first"] < P)).all(): bad.append("first")
    if not bad and walk(d["cells"], d["first"], d["pads"])[1] > CAP: bad.append("places")
    return bad
def reference(cells, first, pads):
    sent, most = walk(cells, first, pads); y = np.zeros((N, 8, 16, N * CAP), np.float32)
    for r in range(N):
        for q in range(N):
            for g in range(8):
                v = sent[q, r, g][0][:, :CAP]; y[r, g, :, q * CAP:q * CAP + v.shape[1]] = v
    return {"y": y.reshape(N, 128, N * CAP)}

@@ -1,0 +1,309 @@
+from concourse.bass import DstId, RemoteDMATransfer
+from concourse.mybir import AluOpType, ActivationFunctionType
+
+N, C, CAP, P = 8, 1024, 160, 8192
+W = N * CAP
+DUMP = 1408
+LIFT = 2048 + DUMP
+EMPTY = 1280
+
+BF, F32, I32, U16 = "bfloat16", "float32", "int32", "uint16"
+
+
+def _sb(n, t):
+    return ("sbuf", [128, n], t)
+
+
+SCRATCH = {
+    "fst": _sb(64, I32), "p0": _sb(512, BF), "cv": _sb(C, BF), "pd": _sb(P, BF),
+    "pi": _sb(8, I32), "pf": _sb(8, F32), "wc": _sb(8, F32), "row": _sb(144, F32), "blk": _sb(128, BF),
+    "onehot": _sb(16, BF), "za": _sb(144, BF), "z0": _sb(144, BF), "zk": _sb(144, BF),
+    "nob": _sb(128, BF), "m1a": _sb(128, BF), "m1": _sb(128, BF), "nid": _sb(128, BF),
+    "dd": _sb(640, F32), "ones": _sb(80, BF),
+    "hi32": _sb(64, I32), "lo32": _sb(64, I32), "hi16": _sb(64, U16), "lo16": _sb(64, U16), "key1": _sb(64, U16),
+    "msk": _sb(C, BF), "gm": _sb(C, BF),
+    "x1": _sb(80, I32), "d1": _sb(80, I32), "e1": _sb(640, BF), "s1": _sb(640, BF), "f1": _sb(640, F32), "o1": _sb(80, U16),
+    "x2": _sb(80, I32), "d2": _sb(80, I32), "e2": _sb(640, BF), "s2": _sb(640, BF), "f2": _sb(640, F32), "o2": _sb(80, U16),
+    "u1": _sb(C, BF), "b1": _sb(C, BF), "nb": _sb(512, BF), "w1": _sb(W, BF), "l1": _sb(W, BF),
+    "xk": _sb(80, I32), "k32": _sb(80, I32), "key2": _sb(80, U16), "v0": _sb(24, I32), "vl": _sb(80, F32),
+    "ub": _sb(W, BF), "ut": _sb(320, BF), "nu": _sb(W, BF), "b2": _sb(W, BF),
+    "w2": _sb(DUMP + W, BF), "l2": _sb(W, BF), "yy": _sb(W, F32),
+    "pt1": ("psum", [128, 512], F32), "pp": ("psum", [128, 1024], F32), "pu": ("psum", [128, 512], F32),
+    "pxa": ("psum", [128, 512], F32), "pxb": ("psum", [128, 512], F32), "pt2": ("psum", [128, 512], F32),
+}
+SEMAPHORES = ["cv_", "ca_", "cp_", "cg_", "ld_f", "ld_0", "ld_c", "ld_p", "st_a", "st_b", "st_c",
+              "a1", "b1", "a2", "b2", "c2", "sent"]
+
+A = AluOpType
+ACT = ActivationFunctionType
+
+
+def emit(g, T, ops, landed):
+    eng = {"v": g.vector, "a": g.scalar, "p": g.tensor, "g": g, "s": g.sync}
+    cnt = {"v": "cv_", "a": "ca_", "p": "cp_", "g": "cg_"}
+    writer = {t: ("x",) + e for t, e in landed.items()}
+    readers = {}
+    known = {q: {} for q in eng}
+    after = []
+    waits = []
+    signal = set()
+    for i, (q, call, rd, wr, dma) in enumerate(ops):
+        need = []
+        for t in rd:
+            if t in writer:
+                need.append(writer[t])
+        for t in wr:
+            if t in writer:
+                need.append(writer[t])
+            need.extend(readers.get(t, []))
+        need.sort(key=lambda e: -e[1] if e[0] == "o" else 1)
+        mine = []
+        for e in need:
+            if e[0] == "x":
+                key, val, more = e[1], e[2], {}
+            else:
+                j = e[1]
+                if ops[j][0] == "p" and q == "p":
+                    continue
+                key, val, more = (ops[j][4], 16, after[j]) if ops[j][4] else (ops[j][0], j, after[j])
+            if known[q].get(key, -1) >= val:
+                continue
+            mine.append(e)
+            known[q][key] = val
+            for k, v in more.items():
+                if known[q].get(k, -1) < v:
+                    known[q][k] = v
+            if e[0] == "o" and not ops[e[1]][4]:
+                signal.add(e[1])
+        waits.append(mine)
+        after.append(dict(known[q]))
+        for t in rd:
+            readers.setdefault(t, []).append(("o", i))
+        for t in wr:
+            writer[t] = ("o", i)
+            readers[t] = []
+    n = {q: 0 for q in cnt}
+    value = {}
+    for i, (q, call, rd, wr, dma) in enumerate(ops):
+        for e in waits[i]:
+            if e[0] == "x":
+                eng[q].wait_ge(T.sem[e[1]], e[2])
+            elif ops[e[1]][4]:
+                eng[q].wait_ge(T.sem[ops[e[1]][4]], 16)
+            else:
+                eng[q].wait_ge(T.sem[cnt[ops[e[1]][0]]], value[e[1]])
+        ins = call(eng[q])
+        if dma:
+            ins.then_inc(T.sem[dma], 16)
+        elif i in signal:
+            n[q] += 1
+            value[i] = n[q]
+            ins.then_inc(T.sem[cnt[q]], 1)
+
+
+def rank_program(g, core, T, topo):
+    me = T.rank_of(core)
+    if me is None:
+        return
+    ops = []
+
+    def op(q, call, rd, wr, dma=None):
+        ops.append((q, call, list(rd), list(wr), dma))
+
+    def ts(out, in0, s1, o0, rd, wr, s2=None, o1=None):
+        if o1 is None:
+            op("v", lambda e: e.tensor_scalar(out, in0, s1, None, o0), rd, wr)
+        else:
+            op("v", lambda e: e.tensor_scalar(out, in0, s1, s2, o0, o1), rd, wr)
+
+    def tt(out, in0, in1, o, rd, wr):
+        op("v", lambda e: e.tensor_tensor(out, in0, in1, o), rd, wr)
+
+    def cp(out, in_, rd, wr):
+        op("v", lambda e: e.tensor_copy(out, in_), rd, wr)
+
+    def fill(out, val, wr):
+        op("v", lambda e: e.memset(out, val), [], wr)
+
+    def act(out, in_, rd, wr, scale=1.0):
+        op("a", lambda e: e.activation(out, in_, ACT.Identity, scale=scale), rd, wr)
+
+    def mm(out, lhs, rhs, start, stop, rd, wr):
+        op("p", lambda e: e.matmul(out, lhs, rhs, start, stop), rd, wr)
+
+    def iota(out, pattern, base, cm, wr, small=True):
+        if small:
+            op("g", lambda e: e.iota(out, pattern, base, cm, allow_small_or_imprecise_dtypes=True), [], wr)
+        else:
+            op("g", lambda e: e.iota(out, pattern, base, cm), [], wr)
+
+    def sel(out, in_, cmp_op, val, rd, wr):
+        op("g", lambda e: e.affine_select(out, in_, [[-1, 128]], cmp_op, val, 0, 1), rd, wr)
+
+    def to_list(out, z, src, c0, c1, start, stop, rd, wr):
+        for r in range(16):
+            mm(out, z[:, 15 - r:143 - r], src[:, c0 + r:c1:16], start and r == 0, stop and r == 15, rd, wr)
+
+    def places(h, n, match, less, between, before_pick):
+        dd, ee, ss, ff, oo = T["d" + h], T["e" + h], T["s" + h], T["f" + h], T["o" + h]
+        et = ["e%s_%d" % (h, d) for d in range(N)]
+        st = ["s%s_%d" % (h, d) for d in range(N)]
+        k = 4 * n
+        for d in range(N):
+            ts(ee[:, d:8 * n:8], dd[:, 0:n], match(d), A.is_equal, ["d" + h], [et[d]])
+        for b in range(2):
+            mm(T.pp[:, 512 - k + b * k:512 + b * k], T.m1[:], ee[:, b * k:b * k + k], True, False, et + ["m1"], ["pp%d" % b])
+        between()
+        for d in range(N):
+            op("v", lambda e, d=d: e.tensor_tensor_scan(ss[:, d:8 * n:8], T.ones[:, 0:n], ee[:, d:8 * n:8],
+                                                        float(128 - 10 * d), A.mult, A.subtract), et + ["ones"], [st[d]])
+        for b in range(2):
+            mm(T.pp[:, 512 - k + b * k:512 + b * k], T.nob[:], ss[:, b * k:b * k + k], False, True, st + ["nob"], ["pp%d" % b])
+        before_pick()
+        for b in range(2):
+            op("v", lambda e, b=b: e.tensor_tensor_scan(ff[:, b * k:b * k + k], T.dd[:, b * k:b * k + k],
+                                                        T.pp[:, 512 - k + b * k:512 + b * k], 8192.0, A.min, A.max),
+               ["dd", "pp%d" % b], ["f%s_%d" % (h, b)])
+        ts(oo[:, 0:n], ff[:, 7:8 * n:8], float(-less), A.add, ["f%s_0" % h, "f%s_1" % h], ["o" + h])
+
+    sent = [0]
+
+    def exchange(win, base, land, sems, rd):
+        for xs, sem in zip(((4, 5, 6, 7), (2, 3), (1,)), sems):
+            tr = []
+            for i, x in enumerate(xs):
+                q = me ^ x
+                dst = T.cores[q]
+                engines = topo.engines(core, dst)
+                k = len(engines) // len(xs)
+                mask = sum(1 << e for e in engines[i * k:(i + 1) * k])
+                rid, pid = topo.addr(dst)[0:2]
+                tr.append((win[:, base + q * CAP:base + (q + 1) * CAP], land[:, me * CAP:(me + 1) * CAP], rid, pid, mask))
+                sent[0] += k
+            if len(tr) == 1:
+                op("g", lambda e, t=tr[0], sem=sem: e.remote_dma(t[1], t[0], T.sem[sem], T.sem.sent, t[3], t[2], t[4]), rd, [])
+            else:
+                op("g", lambda e, tr=tr, sem=sem: e.remote_dma_fused(
+                    [RemoteDMATransfer(dst_ids=[DstId(rid=t[2], pnc=t[3])], dma_engine_mask=t[4], remote_sem=T.sem[sem],
+                                       src=t[0], dst=t[1]) for t in tr], local_sem=T.sem.sent), rd, [])
+
+    per = len(topo.engines(core, T.cores[me ^ 1]))
+    landed = {"l1a": ("a1", per), "l1b": ("b1", 2 * per), "l2a": ("a2", per), "l2b": ("b2", per), "l2c": ("c2", per)}
+
+    op("s", lambda e: e.dma_start(T.p0[:], T.pads[0:128:16, :]), [], ["p0"], "ld_0")
+    op("a", lambda e: e.dma_start(T.fst[:], T.first[:]), [], ["fst"], "ld_f")
+    op("s", lambda e: e.dma_start(T.cv[:], T.cells[:]), [], ["cv"], "ld_c")
+    op("s", lambda e: e.dma_start(T.pd[:], T.pads[:]), [], ["pd"], "ld_p")
+
+    iota(T.pi[:, 2:3], [[0, 1]], 0, 1, ["pi2"], small=False)
+    iota(T.row[:], [[1, 144]], -15, 0, ["row"])
+    iota(T.blk[:], [[16, 8], [0, 16]], 0, 0, ["blk"])
+    ts(T.pi[:, 0:1], T.pi[:, 2:3], 112, A.bitwise_and, ["pi2"], ["pi0"])
+    ts(T.pi[:, 1:2], T.pi[:, 2:3], 15, A.bitwise_and, ["pi2"], ["pi1"])
+    cp(T.pf[:, 0:2], T.pi[:, 0:2], ["pi0", "pi1"], ["pf"])
+    grp, sym = T.pf[:, 0:1], T.pf[:, 1:2]
+    ts(T.wc[:, 0:1], sym, 0.0, A.is_equal, ["pf"], ["wc0"])
+    ts(T.onehot[:], T.row[:, 15:31], sym, A.is_equal, ["row", "pf"], ["onehot"])
+    ts(T.za[:], T.row[:], grp, A.is_equal, ["row", "pf"], ["za"], -1.0, A.mult)
+    ts(T.z0[:], T.row[:], grp, A.is_equal, ["row", "pf", "wc0"], ["z0"], T.wc[:, 0:1], A.mult)
+    ts(T.nob[:], T.blk[:], grp, A.is_equal, ["blk", "pf"], ["nob"], -1.0, A.mult)
+    sel(T.nid[:], T.nob[:], A.is_equal, 0.0, ["nob"], ["nid"])
+    sel(T.m1a[:], T.nob[:], A.is_gt, 0.0, ["nob"], ["m1a"])
+    sel(T.m1[:], T.m1a[:], A.not_equal, float(LIFT), ["m1a"], ["m1"])
+    iota(T.dd[:], [[-16, 80], [8192, 8]], DUMP - 16, -1, ["dd"])
+    iota(T.w1[:], [[0, W]], -EMPTY, 0, ["w1"])
+
+    ts(T.hi32[:], T.fst[:], 9, A.logical_shift_right, ["fst"], ["hi32"])
+    ts(T.lo32[:], T.fst[:], 511, A.bitwise_and, ["fst"], ["lo32"])
+    cp(T.hi16[:], T.hi32[:], ["hi32"], ["hi16"])
+    cp(T.lo16[:], T.lo32[:], ["lo32"], ["lo16"])
+    to_list(T.pt1[:, 0:64], T.z0, T.cv, 0, C, True, False, ["z0", "cv"], ["pt1"])
+    for i in range(4):
+        a, b = 256 * i, 256 * i + 256
+        act(T.msk[:, a:b], T.onehot[:].indirect(T.hi16[:, a // 16:b // 16]), ["onehot", "hi16"], ["msk%d" % i])
+        tt(T.gm[:, a:b], T.p0[:].indirect(T.lo16[:, a // 16:b // 16]), T.msk[:, a:b], A.mult,
+           ["p0", "lo16", "msk%d" % i], ["gm%d" % i])
+    to_list(T.pt1[:, 0:64], T.za, T.gm, 0, C, False, True, ["za", "gm0", "gm1", "gm2", "gm3"], ["pt1"])
+    cp(T.key1[:], T.fst[:], ["fst"], ["key1"])
+    fill(T.ones[:], 1.0, ["ones"])
+    mm(T.pu[:], T.nid[:], T.cv[:, 512:C], True, False, ["nid", "cv"], ["pu"])
+    act(T.nb[:], T.pd[:].indirect(T.key1[:, 32:64]), ["pd", "key1"], ["nb"], -1.0)
+    ts(T.x1[:, 0:64], T.pt1[:, 0:64], 256.0, A.add, ["pt1"], ["x1"])
+    ts(T.d1[:, 0:64], T.x1[:, 0:64], N - 1, A.bitwise_and, ["x1"], ["d1"])
+    places("1", 64, lambda d: float(d), DUMP + 1, lambda: None, lambda: None)
+    mm(T.pu[:], T.nid[:], T.nb[:], False, True, ["nid", "nb"], ["pu"])
+    act(T.u1[:, 512:C], T.pu[:], ["pu"], ["u1b"])
+    tt(T.u1[:, 0:512], T.pd[:].indirect(T.key1[:, 0:32]), T.cv[:, 0:512], A.subtract, ["pd", "key1", "cv"], ["u1a"])
+    for i, h in enumerate("ab"):
+        a, b = 512 * i, 512 * i + 512
+        ts(T.b1[:, a:b], T.u1[:, a:b], 0.0, A.is_gt, ["u1" + h], ["b1" + h], -256.0, A.mult)
+        tt(T.w1[:].indirect(T.o1[:, a // 16:b // 16]), T.u1[:, a:b], T.b1[:, a:b], A.add, ["o1", "u1" + h, "b1" + h], ["w1"])
+    exchange(T.w1, 0, T.l1, ("a1", "b1", "b1"), ["w1"])
+    own = slice(me * CAP, (me + 1) * CAP)
+    act(T.l1[:, own], T.w1[:, own], ["w1"], ["l1o"])
+
+    for i, wgt in enumerate((-65536.0, -1.0, -256.0)):
+        ts(T.wc[:, 1 + i:2 + i], sym, float(i), A.is_equal, ["pf"], ["wc%d" % (1 + i)], wgt, A.mult)
+    fill(T.vl[:], float(EMPTY + 16), ["vl"])
+    ts(T.wc[:, 4:5], T.wc[:, 1:2], T.wc[:, 2:3], A.add, ["wc1", "wc2", "wc3"], ["wc4"], T.wc[:, 3:4], A.add)
+    fill(T.w2[:, DUMP:DUMP + W], 0.0, ["w2"])
+    ts(T.zk[:], T.row[:], grp, A.is_equal, ["row", "pf", "wc4"], ["zk"], T.wc[:, 4:5], A.mult)
+
+    b0 = 640 * (me // 4)
+    a0 = 640 - b0
+    m0 = b0 + 320
+
+    def keys(ps, c0, h):
+        a, b = c0 // 16, c0 // 16 + 40
+        cp(T.xk[:, a:b], ps[:, 0:40], ["px" + h], ["xk" + h])
+        ts(T.k32[:, a:b], T.xk[:, a:b], P - 1, A.bitwise_and, ["xk" + h], ["k32" + h])
+        cp(T.key2[:, a:b], T.k32[:, a:b], ["k32" + h], ["key2" + h])
+
+    def pads_at(a, b):
+        return T.pd[:].indirect(T.key2[:, a // 16:b // 16])
+
+    lb = ["l1b", "l1o"]
+    to_list(T.pxa[:, 0:40], T.zk, T.l1, a0, a0 + 640, True, True, ["zk", "l1a"], ["pxa"])
+    keys(T.pxa, a0, "a")
+    tt(T.ub[:, a0:a0 + 640], pads_at(a0, a0 + 640), T.l1[:, a0:a0 + 640], A.add, ["pd", "key2a", "l1a"], ["uba"])
+    ts(T.b2[:, a0:a0 + 640], T.ub[:, a0:a0 + 640], 0.0, A.is_gt, ["uba"], ["b2a"], 256.0, A.mult)
+    to_list(T.pxb[:, 0:40], T.zk, T.l1, b0, b0 + 640, True, True, ["zk"] + lb, ["pxb"])
+    keys(T.pxb, b0, "b")
+    act(T.ub[:, m0:m0 + 320], pads_at(m0, m0 + 320), ["pd", "key2b"], ["ubm"])
+    tt(T.ub[:, b0:m0], pads_at(b0, m0), T.l1[:, b0:m0], A.add, ["pd", "key2b"] + lb, ["ubb"])
+    to_list(T.pt2[:, a0 // 16:a0 // 16 + 40], T.z0, T.ub, a0, a0 + 640, True, True, ["z0", "uba"], ["pt2"])
+    to_list(T.pt2[:, b0 // 16:b0 // 16 + 40], T.z0, T.ub, b0, b0 + 640, True, True, ["z0", "ubb", "ubm"], ["pt2"])
+    ts(T.v0[:, 0:20], T.xk[:, m0 // 16:m0 // 16 + 20], 16, A.logical_shift_right, ["xkb"], ["v0"])
+    tt(T.ut[:], T.ub[:, m0:m0 + 320], T.l1[:, m0:m0 + 320], A.add, ["ubm"] + lb, ["ut"])
+    ts(T.vl[:, m0 // 16:m0 // 16 + 20], T.v0[:, 0:20], -1.0, A.mult, ["v0"], ["vl"], float(EMPTY + 16), A.add)
+    act(T.nu[:, a0:a0 + 640], T.ub[:, a0:a0 + 640], ["uba"], ["nua"], -1.0)
+    act(T.nu[:, b0:m0], T.ub[:, b0:m0], ["ubb"], ["nub"], -1.0)
+    act(T.nu[:, m0:m0 + 320], T.ut[:], ["ut"], ["num"], -1.0)
+    tt(T.x2[:], T.pt2[:, 0:80], T.vl[:], A.add, ["pt2", "vl"], ["x2"])
+    ts(T.d2[:], T.x2[:], 1024 + N - 1, A.bitwise_and, ["x2"], ["d2"])
+
+    def wraps():
+        ts(T.b2[:, b0:m0], T.ub[:, b0:m0], 0.0, A.is_gt, ["ubb"], ["b2b"], 256.0, A.mult)
+        ts(T.b2[:, m0:m0 + 320], T.ut[:], 0.0, A.is_gt, ["ut"], ["b2m"], 256.0, A.mult)
+
+    places("2", 80, lambda d: float(1024 + (N - d) % N), 1, lambda: None, wraps)
+    tt(T.w2[:].indirect(T.o2[:]), T.nu[:], T.b2[:], A.add, ["o2", "nua", "nub", "num", "b2a", "b2b", "b2m"], ["w2"])
+    exchange(T.w2, DUMP, T.l2, ("a2", "b2", "c2"), ["w2"])
+
+    act(T.yy[:, own], T.w2[:, DUMP + me * CAP:DUMP + (me + 1) * CAP], ["w2"], ["yo"])
+    h0 = a0 + 320
+    act(T.yy[:, a0:h0], T.l2[:, a0:h0], ["l2a"], ["ya0"])
+    cp(T.yy[:, h0:h0 + 320], T.l2[:, h0:h0 + 320], ["l2a"], ["ya1"])
+    op("s", lambda e: e.dma_start(T.y[:, a0:a0 + 640], T.yy[:, a0:a0 + 640]), ["ya0", "ya1"], ["ya"], "st_a")
+    q2 = ((me ^ 2) // 2) * 2 * CAP
+    act(T.yy[:, q2:q2 + 320], T.l2[:, q2:q2 + 320], ["l2b"], ["yb0"])
+    op("a", lambda e: e.dma_start(T.y[:, q2:q2 + 320], T.yy[:, q2:q2 + 320]), ["yb0"], ["yb"], "st_b")
+    q1 = (me ^ 1) * CAP
+    cp(T.yy[:, q1:q1 + CAP], T.l2[:, q1:q1 + CAP], ["l2c"], ["yc0"])
+    q0 = (me // 2) * 2 * CAP
+    op("s", lambda e: e.dma_start(T.y[:, q0:q0 + 320], T.yy[:, q0:q0 + 320]), ["yc0", "yo"], ["yc"], "st_c")
+
+    emit(g, T, ops, landed)
+    for s in ("st_a", "st_b", "st_c"):
+        g.sync.wait_ge(T.sem[s], 16)
+    g.wait_ge(T.sem.sent, sent[0])

@@ -3,9 +3,11 @@ from concourse.mybir import AluOpType, ActivationFunctionType
 
 N, C, CAP, P = 8, 1024, 160, 8192
 W = N * CAP
+H = W // 2
 DUMP = 1408
 LIFT = 2048 + DUMP
 EMPTY = 1280
+BIG = 49152
 
 BF, F32, I32, U16 = "bfloat16", "float32", "int32", "uint16"
 
@@ -14,22 +16,26 @@ def _sb(n, t):
     return ("sbuf", [128, n], t)
 
 
+def _ps(n):
+    return ("psum", [128, n], F32)
+
+
 SCRATCH = {
     "fst": _sb(64, I32), "p0": _sb(512, BF), "cv": _sb(C, BF), "pd": _sb(P, BF),
     "pi": _sb(8, I32), "pf": _sb(8, F32), "wc": _sb(8, F32), "row": _sb(144, F32), "blk": _sb(128, BF),
-    "onehot": _sb(16, BF), "za": _sb(144, BF), "z0": _sb(144, BF), "zk": _sb(144, BF),
+    "onehot": _sb(16, BF), "za": _sb(144, BF), "z0": _sb(144, BF), "zka": _sb(144, BF), "zkb": _sb(144, BF),
     "nob": _sb(128, BF), "m1a": _sb(128, BF), "m1": _sb(128, BF), "nid": _sb(128, BF),
     "dd": _sb(640, F32), "ones": _sb(80, BF),
     "hi32": _sb(64, I32), "lo32": _sb(64, I32), "hi16": _sb(64, U16), "lo16": _sb(64, U16), "key1": _sb(64, U16),
     "msk": _sb(C, BF), "gm": _sb(C, BF),
     "x1": _sb(80, I32), "d1": _sb(80, I32), "e1": _sb(640, BF), "s1": _sb(640, BF), "f1": _sb(640, F32), "o1": _sb(80, U16),
     "x2": _sb(80, I32), "d2": _sb(80, I32), "e2": _sb(640, BF), "s2": _sb(640, BF), "f2": _sb(640, F32), "o2": _sb(80, U16),
-    "u1": _sb(C, BF), "b1": _sb(C, BF), "nb": _sb(512, BF), "w1": _sb(W, BF), "l1": _sb(W, BF),
-    "xk": _sb(80, I32), "k32": _sb(80, I32), "key2": _sb(80, U16), "v0": _sb(24, I32), "vl": _sb(80, F32),
-    "ub": _sb(W, BF), "ut": _sb(320, BF), "nu": _sb(W, BF), "b2": _sb(W, BF),
-    "w2": _sb(DUMP + W, BF), "l2": _sb(W, BF), "yy": _sb(W, F32),
-    "pt1": ("psum", [128, 512], F32), "pp": ("psum", [128, 1024], F32), "pu": ("psum", [128, 512], F32),
-    "pxa": ("psum", [128, 512], F32), "pxb": ("psum", [128, 512], F32), "pt2": ("psum", [128, 512], F32),
+    "nb1": _sb(C, BF), "w1": _sb(W, BF), "l1": _sb(W, BF),
+    "xk": _sb(80, I32), "klo": _sb(40, I32), "khi": _sb(40, I32), "k32": _sb(80, I32), "key2": _sb(80, U16),
+    "v0": _sb(40, I32), "vl": _sb(40, F32), "t1": _sb(H, BF), "w1r": _sb(W, BF),
+    "nb2": _sb(W, BF), "nq": _sb(W, BF), "va": _sb(H, F32), "vb": _sb(H, BF), "tb": _sb(H, BF),
+    "wa": _sb(DUMP + W, F32), "wb": _sb(DUMP + W, BF), "w2": _sb(W, BF), "l2": _sb(W, BF), "yy": _sb(W, F32),
+    "pp": _ps(1024), "pta": _ps(512), "ptb": _ps(512), "pxa": _ps(1024), "pxb": _ps(1024),
 }
 SEMAPHORES = ["cv_", "ca_", "cp_", "cg_", "ld_f", "ld_0", "ld_c", "ld_p", "st_a", "st_b", "st_c",
               "a1", "b1", "a2", "b2", "c2", "sent"]
@@ -122,11 +128,14 @@ def rank_program(g, core, T, topo):
     def cp(out, in_, rd, wr):
         op("v", lambda e: e.tensor_copy(out, in_), rd, wr)
 
+    def scan(out, d0, d1, first, o0, o1, rd, wr):
+        op("v", lambda e: e.tensor_tensor_scan(out, d0, d1, first, o0, o1), rd, wr)
+
     def fill(out, val, wr):
         op("v", lambda e: e.memset(out, val), [], wr)
 
-    def act(out, in_, rd, wr, scale=1.0):
-        op("a", lambda e: e.activation(out, in_, ACT.Identity, scale=scale), rd, wr)
+    def act(out, in_, rd, wr, scale=1.0, bias=0.0, func=ACT.Identity):
+        op("a", lambda e: e.activation(out, in_, func, bias=bias, scale=scale), rd, wr)
 
     def mm(out, lhs, rhs, start, stop, rd, wr):
         op("p", lambda e: e.matmul(out, lhs, rhs, start, stop), rd, wr)
@@ -144,7 +153,7 @@ def rank_program(g, core, T, topo):
         for r in range(16):
             mm(out, z[:, 15 - r:143 - r], src[:, c0 + r:c1:16], start and r == 0, stop and r == 15, rd, wr)
 
-    def places(h, n, match, less, between, before_pick):
+    def places(h, n, match, less, between):
         dd, ee, ss, ff, oo = T["d" + h], T["e" + h], T["s" + h], T["f" + h], T["o" + h]
         et = ["e%s_%d" % (h, d) for d in range(N)]
         st = ["s%s_%d" % (h, d) for d in range(N)]
@@ -153,39 +162,37 @@ def rank_program(g, core, T, topo):
             ts(ee[:, d:8 * n:8], dd[:, 0:n], match(d), A.is_equal, ["d" + h], [et[d]])
         for b in range(2):
             mm(T.pp[:, 512 - k + b * k:512 + b * k], T.m1[:], ee[:, b * k:b * k + k], True, False, et + ["m1"], ["pp%d" % b])
-        between()
         for d in range(N):
-            op("v", lambda e, d=d: e.tensor_tensor_scan(ss[:, d:8 * n:8], T.ones[:, 0:n], ee[:, d:8 * n:8],
-                                                        float(128 - 10 * d), A.mult, A.subtract), et + ["ones"], [st[d]])
+            scan(ss[:, d:8 * n:8], T.ones[:, 0:n], ee[:, d:8 * n:8], float(128 - 10 * d), A.mult, A.subtract,
+                 et[0:4 + d // 4 * 4] + ["ones"], [st[d]])
         for b in range(2):
             mm(T.pp[:, 512 - k + b * k:512 + b * k], T.nob[:], ss[:, b * k:b * k + k], False, True, st + ["nob"], ["pp%d" % b])
-        before_pick()
+        between()
         for b in range(2):
-            op("v", lambda e, b=b: e.tensor_tensor_scan(ff[:, b * k:b * k + k], T.dd[:, b * k:b * k + k],
-                                                        T.pp[:, 512 - k + b * k:512 + b * k], 8192.0, A.min, A.max),
-               ["dd", "pp%d" % b], ["f%s_%d" % (h, b)])
+            scan(ff[:, b * k:b * k + k], T.dd[:, b * k:b * k + k], T.pp[:, 512 - k + b * k:512 + b * k], 8192.0,
+                 A.min, A.max, ["dd", "pp%d" % b], ["f%s_%d" % (h, b)])
         ts(oo[:, 0:n], ff[:, 7:8 * n:8], float(-less), A.add, ["f%s_0" % h, "f%s_1" % h], ["o" + h])
 
     sent = [0]
 
-    def exchange(win, base, land, sems, rd):
-        for xs, sem in zip(((4, 5, 6, 7), (2, 3), (1,)), sems):
-            tr = []
-            for i, x in enumerate(xs):
-                q = me ^ x
-                dst = T.cores[q]
-                engines = topo.engines(core, dst)
-                k = len(engines) // len(xs)
-                mask = sum(1 << e for e in engines[i * k:(i + 1) * k])
-                rid, pid = topo.addr(dst)[0:2]
-                tr.append((win[:, base + q * CAP:base + (q + 1) * CAP], land[:, me * CAP:(me + 1) * CAP], rid, pid, mask))
-                sent[0] += k
-            if len(tr) == 1:
-                op("g", lambda e, t=tr[0], sem=sem: e.remote_dma(t[1], t[0], T.sem[sem], T.sem.sent, t[3], t[2], t[4]), rd, [])
-            else:
-                op("g", lambda e, tr=tr, sem=sem: e.remote_dma_fused(
-                    [RemoteDMATransfer(dst_ids=[DstId(rid=t[2], pnc=t[3])], dma_engine_mask=t[4], remote_sem=T.sem[sem],
-                                       src=t[0], dst=t[1]) for t in tr], local_sem=T.sem.sent), rd, [])
+    def send(win, land, xs, sem, rd):
+        tr = []
+        for i, x in enumerate(xs):
+            q = me ^ x
+            dst = T.cores[q]
+            engines = topo.engines(core, dst)
+            k = len(engines) // len(xs)
+            mask = sum(1 << e for e in engines[i * k:(i + 1) * k])
+            rid, pid = topo.addr(dst)[0:2]
+            tr.append((win[:, q * CAP:(q + 1) * CAP], land[:, me * CAP:(me + 1) * CAP], rid, pid, mask))
+            sent[0] += k
+        if len(tr) == 1:
+            t = tr[0]
+            op("g", lambda e: e.remote_dma(t[1], t[0], T.sem[sem], T.sem.sent, t[3], t[2], t[4]), rd, [])
+        else:
+            op("g", lambda e: e.remote_dma_fused(
+                [RemoteDMATransfer(dst_ids=[DstId(rid=t[2], pnc=t[3])], dma_engine_mask=t[4], remote_sem=T.sem[sem],
+                                   src=t[0], dst=t[1]) for t in tr], local_sem=T.sem.sent), rd, [])
 
     per = len(topo.engines(core, T.cores[me ^ 1]))
     landed = {"l1a": ("a1", per), "l1b": ("b1", 2 * per), "l2a": ("a2", per), "l2b": ("b2", per), "l2c": ("c2", per)}
@@ -217,91 +224,127 @@ def rank_program(g, core, T, topo):
     ts(T.lo32[:], T.fst[:], 511, A.bitwise_and, ["fst"], ["lo32"])
     cp(T.hi16[:], T.hi32[:], ["hi32"], ["hi16"])
     cp(T.lo16[:], T.lo32[:], ["lo32"], ["lo16"])
-    to_list(T.pt1[:, 0:64], T.z0, T.cv, 0, C, True, False, ["z0", "cv"], ["pt1"])
-    for i in range(4):
-        a, b = 256 * i, 256 * i + 256
-        act(T.msk[:, a:b], T.onehot[:].indirect(T.hi16[:, a // 16:b // 16]), ["onehot", "hi16"], ["msk%d" % i])
+    to_list(T.pta[:, 0:64], T.z0, T.cv, 0, C, True, False, ["z0", "cv"], ["pta"])
+    parts = ((0, 256), (256, 640), (640, C))
+    for i, (a, b) in enumerate(parts):
+        hot = T.onehot[:].indirect(T.hi16[:, a // 16:b // 16])
+        (cp if i == 0 else act)(T.msk[:, a:b], hot, ["onehot", "hi16"], ["msk%d" % i])
+        if i == 0:
+            cp(T.key1[:], T.fst[:], ["fst"], ["key1"])
+    for i, (a, b) in enumerate(parts):
         tt(T.gm[:, a:b], T.p0[:].indirect(T.lo16[:, a // 16:b // 16]), T.msk[:, a:b], A.mult,
            ["p0", "lo16", "msk%d" % i], ["gm%d" % i])
-    to_list(T.pt1[:, 0:64], T.za, T.gm, 0, C, False, True, ["za", "gm0", "gm1", "gm2", "gm3"], ["pt1"])
-    cp(T.key1[:], T.fst[:], ["fst"], ["key1"])
+    to_list(T.pta[:, 0:64], T.za, T.gm, 0, C, False, True, ["za", "gm0", "gm1", "gm2"], ["pta"])
     fill(T.ones[:], 1.0, ["ones"])
-    mm(T.pu[:], T.nid[:], T.cv[:, 512:C], True, False, ["nid", "cv"], ["pu"])
-    act(T.nb[:], T.pd[:].indirect(T.key1[:, 32:64]), ["pd", "key1"], ["nb"], -1.0)
-    ts(T.x1[:, 0:64], T.pt1[:, 0:64], 256.0, A.add, ["pt1"], ["x1"])
+    for i in range(2):
+        act(T.nb1[:, 512 * i:512 * i + 512], T.pd[:].indirect(T.key1[:, 32 * i:32 * i + 32]), ["pd", "key1"], ["nb1%d" % i], -1.0)
+    ts(T.x1[:, 0:64], T.pta[:, 0:64], 256.0, A.add, ["pta"], ["x1"])
     ts(T.d1[:, 0:64], T.x1[:, 0:64], N - 1, A.bitwise_and, ["x1"], ["d1"])
-    places("1", 64, lambda d: float(d), DUMP + 1, lambda: None, lambda: None)
-    mm(T.pu[:], T.nid[:], T.nb[:], False, True, ["nid", "nb"], ["pu"])
-    act(T.u1[:, 512:C], T.pu[:], ["pu"], ["u1b"])
-    tt(T.u1[:, 0:512], T.pd[:].indirect(T.key1[:, 0:32]), T.cv[:, 0:512], A.subtract, ["pd", "key1", "cv"], ["u1a"])
-    for i, h in enumerate("ab"):
+    places("1", 64, lambda d: float(d), DUMP + 1, lambda: None)
+    for i in range(2):
         a, b = 512 * i, 512 * i + 512
-        ts(T.b1[:, a:b], T.u1[:, a:b], 0.0, A.is_gt, ["u1" + h], ["b1" + h], -256.0, A.mult)
-        tt(T.w1[:].indirect(T.o1[:, a // 16:b // 16]), T.u1[:, a:b], T.b1[:, a:b], A.add, ["o1", "u1" + h, "b1" + h], ["w1"])
-    exchange(T.w1, 0, T.l1, ("a1", "b1", "b1"), ["w1"])
+        tt(T.w1[:].indirect(T.o1[:, a // 16:b // 16]), T.cv[:, a:b], T.nb1[:, a:b], A.add, ["o1", "cv", "nb1%d" % i], ["w1"])
+    act(T.wa[:, DUMP:DUMP + W], T.pd[:, 0:W], ["pd"], ["wa"], 0.0, 32.0, ACT.Silu)
+    at = {"b": H * (me // 4), "a": H - H * (me // 4)}
+    a0, b0, q2, q0 = at["a"], at["b"], ((me ^ 2) // 2) * 2 * CAP, (me // 2) * 2 * CAP
+    send(T.w1, T.l1, (4, 5, 6, 7), "a1", ["w1"])
+    ts(T.t1[:], T.w1[:, b0:b0 + H], 0.0, A.is_lt, ["w1"], ["t1"], 256.0, A.mult)
+    for c0, xs in ((q2, (2, 3)), (q0, (1,))):
+        tt(T.w1r[:, c0:c0 + 320], T.w1[:, c0:c0 + 320], T.t1[:, c0 - b0:c0 - b0 + 320], A.add, ["w1", "t1"], ["w1r%d" % xs[0]])
+        send(T.w1r, T.l1, xs, "b1", ["w1r%d" % xs[0]])
     own = slice(me * CAP, (me + 1) * CAP)
-    act(T.l1[:, own], T.w1[:, own], ["w1"], ["l1o"])
+    act(T.l1[:, own], T.w1r[:, own], ["w1r1"], ["l1o"])
 
-    for i, wgt in enumerate((-65536.0, -1.0, -256.0)):
-        ts(T.wc[:, 1 + i:2 + i], sym, float(i), A.is_equal, ["pf"], ["wc%d" % (1 + i)], wgt, A.mult)
-    fill(T.vl[:], float(EMPTY + 16), ["vl"])
-    ts(T.wc[:, 4:5], T.wc[:, 1:2], T.wc[:, 2:3], A.add, ["wc1", "wc2", "wc3"], ["wc4"], T.wc[:, 3:4], A.add)
-    fill(T.w2[:, DUMP:DUMP + W], 0.0, ["w2"])
-    ts(T.zk[:], T.row[:], grp, A.is_equal, ["row", "pf", "wc4"], ["zk"], T.wc[:, 4:5], A.mult)
+    for i, (s, wgt) in enumerate(((1, 1.0), (2, 512.0), (2, 256.0), (0, 65536.0))):
+        ts(T.wc[:, 1 + i:2 + i], sym, float(s), A.is_equal, ["pf"], ["wc%d" % (1 + i)], wgt, A.mult)
+    fill(T.wb[:, DUMP:DUMP + W], -1.0 / 32, ["wb"])
+    ts(T.wc[:, 5:6], T.wc[:, 1:2], T.wc[:, 2:3], A.add, ["wc1", "wc2"], ["wc5"])
+    ts(T.wc[:, 6:7], T.wc[:, 1:2], T.wc[:, 3:4], A.add, ["wc1", "wc3", "wc4"], ["wc6"], T.wc[:, 4:5], A.add)
+    ts(T.zka[:], T.row[:], grp, A.is_equal, ["row", "pf", "wc5"], ["zka"], T.wc[:, 5:6], A.mult)
+    ts(T.zkb[:], T.row[:], grp, A.is_equal, ["row", "pf", "wc6"], ["zkb"], T.wc[:, 6:7], A.mult)
 
-    b0 = 640 * (me // 4)
-    a0 = 640 - b0
-    m0 = b0 + 320
+    came = {"a": ["l1a"], "b": ["l1b", "l1o"]}
+    ca, cb = slice(a0 // 16, a0 // 16 + 40), slice(b0 // 16, b0 // 16 + 40)
+    pka, pkb = T.pp[:, 0:40], T.pp[:, 984:1024]
 
-    def keys(ps, c0, h):
-        a, b = c0 // 16, c0 // 16 + 40
-        cp(T.xk[:, a:b], ps[:, 0:40], ["px" + h], ["xk" + h])
-        ts(T.k32[:, a:b], T.xk[:, a:b], P - 1, A.bitwise_and, ["xk" + h], ["k32" + h])
-        cp(T.key2[:, a:b], T.k32[:, a:b], ["k32" + h], ["key2" + h])
+    def pads(h):
+        a, m, b = at[h], at[h] + H // 2, at[h] + H
+        act(T.nb2[:, a:m], T.pd[:].indirect(T.key2[:, a // 16:m // 16]), ["pd", "key2" + h], ["nb0" + h], -1.0)
+        ts(T.nb2[:, m:b], T.pd[:].indirect(T.key2[:, m // 16:b // 16]), -1.0, A.mult, ["pd", "key2" + h], ["nb1" + h])
 
-    def pads_at(a, b):
-        return T.pd[:].indirect(T.key2[:, a // 16:b // 16])
+    def px(h, i):
+        return T["px" + h][:, 512 * i:512 * i + H // 2]
 
-    lb = ["l1b", "l1o"]
-    to_list(T.pxa[:, 0:40], T.zk, T.l1, a0, a0 + 640, True, True, ["zk", "l1a"], ["pxa"])
-    keys(T.pxa, a0, "a")
-    tt(T.ub[:, a0:a0 + 640], pads_at(a0, a0 + 640), T.l1[:, a0:a0 + 640], A.add, ["pd", "key2a", "l1a"], ["uba"])
-    ts(T.b2[:, a0:a0 + 640], T.ub[:, a0:a0 + 640], 0.0, A.is_gt, ["uba"], ["b2a"], 256.0, A.mult)
-    to_list(T.pxb[:, 0:40], T.zk, T.l1, b0, b0 + 640, True, True, ["zk"] + lb, ["pxb"])
-    keys(T.pxb, b0, "b")
-    act(T.ub[:, m0:m0 + 320], pads_at(m0, m0 + 320), ["pd", "key2b"], ["ubm"])
-    tt(T.ub[:, b0:m0], pads_at(b0, m0), T.l1[:, b0:m0], A.add, ["pd", "key2b"] + lb, ["ubb"])
-    to_list(T.pt2[:, a0 // 16:a0 // 16 + 40], T.z0, T.ub, a0, a0 + 640, True, True, ["z0", "uba"], ["pt2"])
-    to_list(T.pt2[:, b0 // 16:b0 // 16 + 40], T.z0, T.ub, b0, b0 + 640, True, True, ["z0", "ubb", "ubm"], ["pt2"])
-    ts(T.v0[:, 0:20], T.xk[:, m0 // 16:m0 // 16 + 20], 16, A.logical_shift_right, ["xkb"], ["v0"])
-    tt(T.ut[:], T.ub[:, m0:m0 + 320], T.l1[:, m0:m0 + 320], A.add, ["ubm"] + lb, ["ut"])
-    ts(T.vl[:, m0 // 16:m0 // 16 + 20], T.v0[:, 0:20], -1.0, A.mult, ["v0"], ["vl"], float(EMPTY + 16), A.add)
-    act(T.nu[:, a0:a0 + 640], T.ub[:, a0:a0 + 640], ["uba"], ["nua"], -1.0)
-    act(T.nu[:, b0:m0], T.ub[:, b0:m0], ["ubb"], ["nub"], -1.0)
-    act(T.nu[:, m0:m0 + 320], T.ut[:], ["ut"], ["num"], -1.0)
-    tt(T.x2[:], T.pt2[:, 0:80], T.vl[:], A.add, ["pt2", "vl"], ["x2"])
-    ts(T.d2[:], T.x2[:], 1024 + N - 1, A.bitwise_and, ["x2"], ["d2"])
+    def part(buf, h, i):
+        return buf[:, at[h] + i * H // 2:at[h] + (i + 1) * H // 2]
 
-    def wraps():
-        ts(T.b2[:, b0:m0], T.ub[:, b0:m0], 0.0, A.is_gt, ["ubb"], ["b2b"], 256.0, A.mult)
-        ts(T.b2[:, m0:m0 + 320], T.ut[:], 0.0, A.is_gt, ["ut"], ["b2m"], 256.0, A.mult)
+    def minus(h, src, start, stop, rd, which=(0, 1)):
+        for i in which:
+            mm(px(h, i), T.nid[:], part(src, h, i), start, stop, ["nid"] + rd, ["px%s%d" % (h, i)])
 
-    places("2", 80, lambda d: float(1024 + (N - d) % N), 1, lambda: None, wraps)
-    tt(T.w2[:].indirect(T.o2[:]), T.nu[:], T.b2[:], A.add, ["o2", "nua", "nub", "num", "b2a", "b2b", "b2m"], ["w2"])
-    exchange(T.w2, DUMP, T.l2, ("a2", "b2", "c2"), ["w2"])
+    def dests(h):
+        to_list(T["pt" + h][:, 0:40], T.z0, T.nb2, at[h], at[h] + H, h == "b", True, ["z0", "nb0" + h, "nb1" + h], ["pt" + h])
+        minus(h, T.nb2, False, True, ["nb0" + h, "nb1" + h])
 
-    act(T.yy[:, own], T.w2[:, DUMP + me * CAP:DUMP + (me + 1) * CAP], ["w2"], ["yo"])
-    h0 = a0 + 320
-    act(T.yy[:, a0:h0], T.l2[:, a0:h0], ["l2a"], ["ya0"])
-    cp(T.yy[:, h0:h0 + 320], T.l2[:, h0:h0 + 320], ["l2a"], ["ya1"])
-    op("s", lambda e: e.dma_start(T.y[:, a0:a0 + 640], T.yy[:, a0:a0 + 640]), ["ya0", "ya1"], ["ya"], "st_a")
-    q2 = ((me ^ 2) // 2) * 2 * CAP
-    act(T.yy[:, q2:q2 + 320], T.l2[:, q2:q2 + 320], ["l2b"], ["yb0"])
-    op("a", lambda e: e.dma_start(T.y[:, q2:q2 + 320], T.yy[:, q2:q2 + 320]), ["yb0"], ["yb"], "st_b")
+    to_list(pka, T.zka, T.l1, a0, a0 + H, True, True, ["zka", "l1a"], ["pp0"])
+    to_list(T.pta[:, 0:40], T.z0, T.l1, a0, a0 + H, True, False, ["z0", "l1a"], ["pta"])
+    minus("a", T.l1, True, False, came["a"])
+    ts(T.xk[:, ca], pka, float(256 + 512 * 256), A.add, ["pp0"], ["xka"])
+    ts(T.klo[:], T.xk[:, ca], 255, A.bitwise_and, ["xka"], ["klo"])
+    ts(T.khi[:], T.xk[:, ca], 1, A.arith_shift_right, ["xka"], ["khi"], P - 256, A.bitwise_and)
+    tt(T.k32[:, ca], T.klo[:], T.khi[:], A.add, ["klo", "khi"], ["k32a"])
+    cp(T.key2[:, ca], T.k32[:, ca], ["k32a"], ["key2a"])
+    pads("a")
+    to_list(pkb, T.zkb, T.l1, b0, b0 + H, True, True, ["zkb"] + came["b"], ["pp1"])
+    cp(T.xk[:, cb], pkb, ["pp1"], ["xkb"])
+    ts(T.k32[:, cb], T.xk[:, cb], P - 1, A.bitwise_and, ["xkb"], ["k32b"])
+    cp(T.key2[:, cb], T.k32[:, cb], ["k32b"], ["key2b"])
+    pads("b")
+    dests("a")
+    minus("b", T.l1, True, False, came["b"])
+    dests("b")
+    ts(T.v0[:], T.xk[:, cb], 16, A.arith_shift_right, ["xkb"], ["v0"])
+    ts(T.x2[:, ca], T.pta[:, 0:40], 1536.0, A.add, ["pta"], ["x2a"])
+    ts(T.vl[:], T.v0[:], 1536.0, A.add, ["v0"], ["vl"])
+    ts(part(T.nq, "a", 0), px("a", 0), 127.5 - BIG, A.add, ["pxa0"], ["nqa0"])
+    act(part(T.nq, "a", 1), px("a", 1), ["pxa1"], ["nqa1"], 1.0, 127.5 - BIG)
+    for i in range(2):
+        act(T.vb[:, i * H // 2:(i + 1) * H // 2], px("b", i), ["pxb%d" % i], ["vb%d" % i], 1.0 / 32, -1.0 / 32)
+    for i in range(2):
+        minus("a", T.l1, True, False, came["a"], (i,))
+        minus("a", T.nb2, False, False, ["nb0a", "nb1a"], (i,))
+        minus("a", T.nq, False, True, ["nqa%d" % i], (i,))
+        act(T.va[:, i * H // 2:(i + 1) * H // 2], px("a", i), ["pxa%d" % i], ["va%d" % i], -32.0, 32.0 * (BIG + 1))
+    tt(T.x2[:, cb], T.ptb[:, 0:40], T.vl[:], A.add, ["ptb", "vl"], ["x2b"])
+    ts(T.d2[:], T.x2[:], 1024 + N - 1, A.bitwise_and, ["x2a", "x2b"], ["d2"])
+    places("2", 80, lambda d: float(1024 + d), 1,
+           lambda: ts(T.tb[:], T.vb[:], 0.0, A.is_ge, ["vb0", "vb1"], ["tb"], -8.0, A.mult))
+    op("a", lambda e: e.activation(T.wa[:].indirect(T.o2[:, ca]), T.va[:], ACT.Silu), ["o2", "va0", "va1"], ["wa"])
+    tt(T.wb[:].indirect(T.o2[:, cb]), T.vb[:], T.tb[:], A.add, ["o2", "vb0", "vb1", "tb"], ["wb"])
+
+    for c0, n, xs, sem in ((q2, 320, (2, 3), "b2"), (a0, H, (4, 5, 6, 7), "a2"), (q0, 320, (1,), "c2")):
+        scan(T.w2[:, c0:c0 + n], T.wa[:, DUMP + c0:DUMP + c0 + n], T.wb[:, DUMP + c0:DUMP + c0 + n], -1.0, A.max, A.mult,
+             ["wa", "wb"], ["w2" + sem])
+        send(T.w2, T.l2, xs, sem, ["w2" + sem])
+
+    def widen(q, src, a, b, rd, wr):
+        if q == "a":
+            act(T.yy[:, a:b], src[:, a:b], rd, wr, -1.0, -1.0)
+        else:
+            ts(T.yy[:, a:b], src[:, a:b], -1.0, A.mult, rd, wr, -1.0, A.add)
+
+    def store(q, a, b, rd, sem):
+        op(q, lambda e: e.dma_start(T.y[:, a:b], T.yy[:, a:b]), rd, [], sem)
+
+    widen("a", T.w2, me * CAP, (me + 1) * CAP, ["w2c2"], ["yo"])
+    widen("a", T.l2, q2, q2 + 320, ["l2b"], ["yb"])
+    store("a", q2, q2 + 320, ["yb"], "st_b")
+    widen("v", T.l2, a0, a0 + 320, ["l2a"], ["ya0"])
+    widen("a", T.l2, a0 + 320, a0 + H, ["l2a"], ["ya1"])
+    store("s", a0, a0 + H, ["ya0", "ya1"], "st_a")
     q1 = (me ^ 1) * CAP
-    cp(T.yy[:, q1:q1 + CAP], T.l2[:, q1:q1 + CAP], ["l2c"], ["yc0"])
-    q0 = (me // 2) * 2 * CAP
-    op("s", lambda e: e.dma_start(T.y[:, q0:q0 + 320], T.yy[:, q0:q0 + 320]), ["yc0", "yo"], ["yc"], "st_c")
+    widen("v", T.l2, q1, q1 + CAP, ["l2c"], ["yc"])
+    store("a", q0, q0 + 320, ["yc", "yo"], "st_c")
 
     emit(g, T, ops, landed)
     for s in ("st_a", "st_b", "st_c"):

@@ -6,10 +6,12 @@ W = N * CAP
 H = W // 2
 DUMP = 1408
 LIFT = 2048 + DUMP
-EMPTY = 1280
+NS = 416
+FILL = 2.0 ** 20
+SEG = 20 + CAP
 BIG = 49152
 
-BF, F32, I32, U16 = "bfloat16", "float32", "int32", "uint16"
+BF, F16, F32, I32, U16 = "bfloat16", "float16", "float32", "int32", "uint16"
 
 
 def _sb(n, t):
@@ -23,22 +25,23 @@ def _ps(n):
 SCRATCH = {
     "fst": _sb(64, I32), "p0": _sb(512, BF), "cv": _sb(C, BF), "pd": _sb(P, BF),
     "pi": _sb(8, I32), "pf": _sb(8, F32), "wc": _sb(8, F32), "row": _sb(144, F32), "blk": _sb(128, BF),
-    "onehot": _sb(16, BF), "za": _sb(144, BF), "z0": _sb(144, BF), "zka": _sb(144, BF), "zkb": _sb(144, BF),
+    "onehot": _sb(16, BF), "za": _sb(144, BF), "z0": _sb(144, BF), "zk": _sb(144, BF),
     "nob": _sb(128, BF), "m1a": _sb(128, BF), "m1": _sb(128, BF), "nid": _sb(128, BF),
-    "dd": _sb(640, F32), "ones": _sb(80, BF),
+    "dd": _sb(640, F32), "ones": _sb(144, BF), "z8": _sb(144, BF), "c0": _sb(C, BF),
     "hi32": _sb(64, I32), "lo32": _sb(64, I32), "hi16": _sb(64, U16), "lo16": _sb(64, U16), "key1": _sb(64, U16),
     "msk": _sb(C, BF), "gm": _sb(C, BF),
     "x1": _sb(80, I32), "d1": _sb(80, I32), "e1": _sb(640, BF), "s1": _sb(640, BF), "f1": _sb(640, F32), "o1": _sb(80, U16),
     "x2": _sb(80, I32), "d2": _sb(80, I32), "e2": _sb(640, BF), "s2": _sb(640, BF), "f2": _sb(640, F32), "o2": _sb(80, U16),
-    "nb1": _sb(C, BF), "w1": _sb(W, BF), "l1": _sb(W, BF),
-    "xk": _sb(80, I32), "klo": _sb(40, I32), "khi": _sb(40, I32), "k32": _sb(80, I32), "key2": _sb(80, U16),
-    "v0": _sb(40, I32), "vl": _sb(40, F32), "t1": _sb(H, BF), "w1r": _sb(W, BF),
+    "nb1": _sb(C, BF), "cs": _sb(C, BF), "va1": _sb(NS, F32), "ws1": _sb(W, F32), "wd1": _sb(W, BF), "w1": _sb(W, F16), "l1": _sb(W, F16),
+    "xk": _sb(80, I32), "klo": _sb(80, I32), "khi": _sb(80, I32), "k32": _sb(80, I32), "key2": _sb(40, U16),
+    "su": ("sbuf", [128, N, SEG], U16), "lu": ("sbuf", [128, N, SEG], U16),
+    "vl": _sb(80, F32), "t1": _sb(W, BF),
     "nb2": _sb(W, BF), "nq": _sb(W, BF), "va": _sb(H, F32), "vb": _sb(H, BF), "tb": _sb(H, BF),
     "wa": _sb(DUMP + W, F32), "wb": _sb(DUMP + W, BF), "w2": _sb(W, BF), "l2": _sb(W, BF), "yy": _sb(W, F32),
-    "pp": _ps(1024), "pta": _ps(512), "ptb": _ps(512), "pxa": _ps(1024), "pxb": _ps(1024),
+    "pp": _ps(1024), "pt": _ps(512), "pxa": _ps(1024), "pxb": _ps(1024),
 }
-SEMAPHORES = ["cv_", "ca_", "cp_", "cg_", "ld_f", "ld_0", "ld_c", "ld_p", "st_a", "st_b", "st_c",
-              "a1", "b1", "a2", "b2", "c2", "sent"]
+SEMAPHORES = ["cv_", "ca_", "cp_", "cg_", "ld_f", "ld_0", "ld_1", "ld_c", "ld_p", "st_a", "st_b", "st_c",
+              "m1", "a1", "b1", "m2", "a2", "b2", "sent"]
 
 A = AluOpType
 ACT = ActivationFunctionType
@@ -153,29 +156,38 @@ def rank_program(g, core, T, topo):
         for r in range(16):
             mm(out, z[:, 15 - r:143 - r], src[:, c0 + r:c1:16], start and r == 0, stop and r == 15, rd, wr)
 
-    def places(h, n, match, less, between):
-        dd, ee, ss, ff, oo = T["d" + h], T["e" + h], T["s" + h], T["f" + h], T["o" + h]
-        et = ["e%s_%d" % (h, d) for d in range(N)]
+    def marks(h, a, b, mask, match, tag, between=lambda: None):
+        ts(T["d" + h][:, a:b], T["x" + h][:, a:b], mask, A.bitwise_and, ["x" + tag], ["d" + tag])
+        between()
+        for d in range(N):
+            ts(T["e" + h][:, 8 * a + d:8 * b:8], T["d" + h][:, a:b], match(d), A.is_equal, ["d" + tag], ["e%s_%d" % (tag, d)])
+
+    def places(h, n, last, less, between):
+        ee, ss, ff, oo = T["e" + h], T["s" + h], T["f" + h], T["o" + h]
+        et = ["e%s_%d" % (last, d) for d in range(N)]
         st = ["s%s_%d" % (h, d) for d in range(N)]
         k = 4 * n
-        for d in range(N):
-            ts(ee[:, d:8 * n:8], dd[:, 0:n], match(d), A.is_equal, ["d" + h], [et[d]])
         for b in range(2):
             mm(T.pp[:, 512 - k + b * k:512 + b * k], T.m1[:], ee[:, b * k:b * k + k], True, False, et + ["m1"], ["pp%d" % b])
         for d in range(N):
             scan(ss[:, d:8 * n:8], T.ones[:, 0:n], ee[:, d:8 * n:8], float(128 - 10 * d), A.mult, A.subtract,
                  et[0:4 + d // 4 * 4] + ["ones"], [st[d]])
         for b in range(2):
+            between[b]()
             mm(T.pp[:, 512 - k + b * k:512 + b * k], T.nob[:], ss[:, b * k:b * k + k], False, True, st + ["nob"], ["pp%d" % b])
-        between()
+        between[2]()
         for b in range(2):
             scan(ff[:, b * k:b * k + k], T.dd[:, b * k:b * k + k], T.pp[:, 512 - k + b * k:512 + b * k], 8192.0,
                  A.min, A.max, ["dd", "pp%d" % b], ["f%s_%d" % (h, b)])
-        ts(oo[:, 0:n], ff[:, 7:8 * n:8], float(-less), A.add, ["f%s_0" % h, "f%s_1" % h], ["o" + h])
+        for b in range(2):
+            ts(oo[:, b * n // 2:(b + 1) * n // 2], ff[:, b * k + 7:b * k + k:8], float(-less), A.add,
+               ["f%s_%d" % (h, b)], ["o%s_%d" % (h, b)])
+            if b == 0:
+                between[3]()
 
     sent = [0]
 
-    def send(win, land, xs, sem, rd):
+    def send(win, land, xs, sem, rd, seg=CAP):
         tr = []
         for i, x in enumerate(xs):
             q = me ^ x
@@ -184,24 +196,27 @@ def rank_program(g, core, T, topo):
             k = len(engines) // len(xs)
             mask = sum(1 << e for e in engines[i * k:(i + 1) * k])
             rid, pid = topo.addr(dst)[0:2]
-            tr.append((win[:, q * CAP:(q + 1) * CAP], land[:, me * CAP:(me + 1) * CAP], rid, pid, mask))
+            if seg:
+                tr.append((win[:, q * seg:(q + 1) * seg], land[:, me * seg:(me + 1) * seg], rid, pid, mask))
+            else:
+                tr.append((win[:, q, :], land[:, me, :], rid, pid, mask))
             sent[0] += k
-        if len(tr) == 1:
-            t = tr[0]
-            op("g", lambda e: e.remote_dma(t[1], t[0], T.sem[sem], T.sem.sent, t[3], t[2], t[4]), rd, [])
-        else:
-            op("g", lambda e: e.remote_dma_fused(
-                [RemoteDMATransfer(dst_ids=[DstId(rid=t[2], pnc=t[3])], dma_engine_mask=t[4], remote_sem=T.sem[sem],
-                                   src=t[0], dst=t[1]) for t in tr], local_sem=T.sem.sent), rd, [])
+        op("g", lambda e: e.remote_dma_fused(
+            [RemoteDMATransfer(dst_ids=[DstId(rid=t[2], pnc=t[3])], dma_engine_mask=t[4], remote_sem=T.sem[sem],
+                               src=t[0], dst=t[1]) for t in tr], local_sem=T.sem.sent), rd, [])
 
     per = len(topo.engines(core, T.cores[me ^ 1]))
-    landed = {"l1a": ("a1", per), "l1b": ("b1", 2 * per), "l2a": ("a2", per), "l2b": ("b2", per), "l2c": ("c2", per)}
+    landed = {"l10": ("m1", per), "l12": ("a1", per), "lub": ("b1", per), "l2m": ("m2", per), "l2a": ("a2", per), "l2b": ("b2", per)}
 
+    op("s", lambda e: e.dma_start(T.fst[:], T.first[:]), [], ["fst"], "ld_f")
     op("s", lambda e: e.dma_start(T.p0[:], T.pads[0:128:16, :]), [], ["p0"], "ld_0")
-    op("a", lambda e: e.dma_start(T.fst[:], T.first[:]), [], ["fst"], "ld_f")
-    op("s", lambda e: e.dma_start(T.cv[:], T.cells[:]), [], ["cv"], "ld_c")
+    op("s", lambda e: e.dma_start(T.c0[0:8, :], T.cells[0:128:16, :]), [], ["c0"], "ld_1")
     op("s", lambda e: e.dma_start(T.pd[:], T.pads[:]), [], ["pd"], "ld_p")
+    op("s", lambda e: e.dma_start(T.cv[:], T.cells[:]), [], ["cv"], "ld_c")
 
+    fill(T.ones[:], 1.0, ["ones"])
+    act(T.ws1[:, 0:144], T.ones[:], ["ones"], ["ws1a"], FILL, 0.0, ACT.Silu)
+    fill(T.wd1[:], -1.0 / 1024, ["wd1"])
     iota(T.pi[:, 2:3], [[0, 1]], 0, 1, ["pi2"], small=False)
     iota(T.row[:], [[1, 144]], -15, 0, ["row"])
     iota(T.blk[:], [[16, 8], [0, 16]], 0, 0, ["blk"])
@@ -214,18 +229,20 @@ def rank_program(g, core, T, topo):
     ts(T.za[:], T.row[:], grp, A.is_equal, ["row", "pf"], ["za"], -1.0, A.mult)
     ts(T.z0[:], T.row[:], grp, A.is_equal, ["row", "pf", "wc0"], ["z0"], T.wc[:, 0:1], A.mult)
     ts(T.nob[:], T.blk[:], grp, A.is_equal, ["blk", "pf"], ["nob"], -1.0, A.mult)
+    op("g", lambda e: e.affine_select(T.z8[0:8, :], T.ones[0:8, :], [[1, 144]], A.is_equal, 0.0, -15, -16), ["ones"], ["z8"])
     sel(T.nid[:], T.nob[:], A.is_equal, 0.0, ["nob"], ["nid"])
     sel(T.m1a[:], T.nob[:], A.is_gt, 0.0, ["nob"], ["m1a"])
     sel(T.m1[:], T.m1a[:], A.not_equal, float(LIFT), ["m1a"], ["m1"])
     iota(T.dd[:], [[-16, 80], [8192, 8]], DUMP - 16, -1, ["dd"])
-    iota(T.w1[:], [[0, W]], -EMPTY, 0, ["w1"])
+    iota(T.ws1[:, 144:W], [[0, W - 144]], int(FILL), 0, ["ws1b"])
 
     ts(T.hi32[:], T.fst[:], 9, A.logical_shift_right, ["fst"], ["hi32"])
     ts(T.lo32[:], T.fst[:], 511, A.bitwise_and, ["fst"], ["lo32"])
     cp(T.hi16[:], T.hi32[:], ["hi32"], ["hi16"])
     cp(T.lo16[:], T.lo32[:], ["lo32"], ["lo16"])
-    to_list(T.pta[:, 0:64], T.z0, T.cv, 0, C, True, False, ["z0", "cv"], ["pta"])
-    parts = ((0, 256), (256, 640), (640, C))
+    for r in range(16):
+        mm(T.pt[:, 0:64], T.z8[0:8, 15 - r:143 - r], T.c0[0:8, r:C:16], r == 0, False, ["z8", "c0"], ["pt"])
+    parts = ((0, 192), (192, 576), (576, C))
     for i, (a, b) in enumerate(parts):
         hot = T.onehot[:].indirect(T.hi16[:, a // 16:b // 16])
         (cp if i == 0 else act)(T.msk[:, a:b], hot, ["onehot", "hi16"], ["msk%d" % i])
@@ -234,98 +251,162 @@ def rank_program(g, core, T, topo):
     for i, (a, b) in enumerate(parts):
         tt(T.gm[:, a:b], T.p0[:].indirect(T.lo16[:, a // 16:b // 16]), T.msk[:, a:b], A.mult,
            ["p0", "lo16", "msk%d" % i], ["gm%d" % i])
-    to_list(T.pta[:, 0:64], T.za, T.gm, 0, C, False, True, ["za", "gm0", "gm1", "gm2"], ["pta"])
-    fill(T.ones[:], 1.0, ["ones"])
-    for i in range(2):
-        act(T.nb1[:, 512 * i:512 * i + 512], T.pd[:].indirect(T.key1[:, 32 * i:32 * i + 32]), ["pd", "key1"], ["nb1%d" % i], -1.0)
-    ts(T.x1[:, 0:64], T.pta[:, 0:64], 256.0, A.add, ["pta"], ["x1"])
-    ts(T.d1[:, 0:64], T.x1[:, 0:64], N - 1, A.bitwise_and, ["x1"], ["d1"])
-    places("1", 64, lambda d: float(d), DUMP + 1, lambda: None)
-    for i in range(2):
-        a, b = 512 * i, 512 * i + 512
-        tt(T.w1[:].indirect(T.o1[:, a // 16:b // 16]), T.cv[:, a:b], T.nb1[:, a:b], A.add, ["o1", "cv", "nb1%d" % i], ["w1"])
+    to_list(T.pt[:, 0:64], T.za, T.gm, 0, C, False, True, ["za", "gm0", "gm1", "gm2"], ["pt"])
+    act(T.wb[:, DUMP:DUMP + W], T.wd1[:], ["wd1"], ["wb"], 32.0)
+    na = C - NS
+    mid = na // 64 * 32
+    px1 = T.pxb[:, 0:NS]
+    for i, wgt in enumerate((-1.0, -1024.0)):
+        ts(T.wc[:, 1 + i:2 + i], sym, float(1 + i), A.is_equal, ["pf"], ["wc%d" % (1 + i)], wgt, A.mult)
+    ts(T.wc[:, 3:4], T.wc[:, 1:2], T.wc[:, 2:3], A.add, ["wc1", "wc2"], ["wc3"])
+    ts(T.zk[:], T.row[:], grp, A.is_equal, ["row", "pf", "wc3"], ["zk"], T.wc[:, 3:4], A.mult)
+
+    def scaled(i, a, b):
+        ts(T.cs[:, a:b], T.cv[:, a:b], 1.0, A.add, ["cv"], ["cs%d" % i], -1.0 / FILL, A.mult)
+
+    def pads1(a, b, scale, tag):
+        act(T.nb1[:, a:b], T.pd[:].indirect(T.key1[:, a // 16:b // 16]), ["pd", "key1"], [tag], scale)
+
+    pads1(na, C, -1.0, "nb1s")
+    pads1(0, mid, 1.0 / FILL, "nb10")
+    ts(T.x1[:, 0:64], T.pt[:, 0:64], 256.0, A.add, ["pt"], ["x1"])
+    marks("1", 0, 64, N - 1, lambda d: float(d), "1")
+
+    def reduce1():
+        mm(px1, T.nid[:], T.nb1[:, na:C], True, False, ["nid", "nb1s"], ["bank2"])
+        mm(px1, T.nid[:], T.cv[:, na:C], False, True, ["nid", "cv"], ["bank2"])
+        pads1(mid, na, 1.0 / FILL, "nb11")
+        act(T.va1[:], px1, ["bank2"], ["va1"], -1024.0, 1024.0 * 257)
+
+    places("1", 64, "1", DUMP + 1, [lambda: None, lambda: None, reduce1, lambda: scaled(0, 0, mid)])
+    op("a", lambda e: e.activation(T.ws1[:].indirect(T.o1[:, na // 16:C // 16]), T.va1[:], ACT.Silu),
+       ["o1_1", "va1"], ["ws1a", "ws1b"])
+    for i, (a, b) in enumerate(((0, mid), (mid, na))):
+        if i:
+            scaled(i, a, b)
+        tt(T.wd1[:].indirect(T.o1[:, a // 16:b // 16]), T.cs[:, a:b], T.nb1[:, a:b], A.add,
+           ["o1_0", "o1_%d" % i, "cs%d" % i, "nb1%d" % i], ["wd1"])
+    a0 = H * (me // 4)
+    b0 = H - a0
+    pair = {x: ((me ^ x) // 2) * 2 * CAP for x in (0, 2, 4, 6)}
+
+    def merge1(out, a, n, tag):
+        scan(out[:, a:a + n], T.ws1[:, a:a + n], T.wd1[:, a:a + n], -1.0, A.max, A.mult, ["ws1a", "ws1b", "wd1"], [tag])
+
+    merge1(T.w1, (me ^ 1) * CAP, CAP, "w11")
+    send(T.w1, T.l1, (1,), "m1", ["w11"])
+    bank = [T.pxa[:, 0:320], T.pxa[:, 512:832], T.pxb[:, 0:320], T.pxb[:, 512:832]]
+
+    def part(buf, x, off=0):
+        return buf[:, pair[x] - off:pair[x] - off + 320]
+
+    def minus(i, x, src, start, stop, rd):
+        mm(bank[i], T.nid[:], part(src, x), start, stop, ["nid"] + rd, ["bank%d" % i])
+
+    merge1(T.w1, b0, H, "w1b")
+    merge1(T.w1, pair[2], 320, "w12")
+    send(T.w1, T.l1, (2, 3), "a1", ["w12"])
     act(T.wa[:, DUMP:DUMP + W], T.pd[:, 0:W], ["pd"], ["wa"], 0.0, 32.0, ACT.Silu)
-    at = {"b": H * (me // 4), "a": H - H * (me // 4)}
-    a0, b0, q2, q0 = at["a"], at["b"], ((me ^ 2) // 2) * 2 * CAP, (me // 2) * 2 * CAP
-    send(T.w1, T.l1, (4, 5, 6, 7), "a1", ["w1"])
-    ts(T.t1[:], T.w1[:, b0:b0 + H], 0.0, A.is_lt, ["w1"], ["t1"], 256.0, A.mult)
-    for c0, xs in ((q2, (2, 3)), (q0, (1,))):
-        tt(T.w1r[:, c0:c0 + 320], T.w1[:, c0:c0 + 320], T.t1[:, c0 - b0:c0 - b0 + 320], A.add, ["w1", "t1"], ["w1r%d" % xs[0]])
-        send(T.w1r, T.l1, xs, "b1", ["w1r%d" % xs[0]])
-    own = slice(me * CAP, (me + 1) * CAP)
-    act(T.l1[:, own], T.w1r[:, own], ["w1r1"], ["l1o"])
 
-    for i, (s, wgt) in enumerate(((1, 1.0), (2, 512.0), (2, 256.0), (0, 65536.0))):
-        ts(T.wc[:, 1 + i:2 + i], sym, float(s), A.is_equal, ["pf"], ["wc%d" % (1 + i)], wgt, A.mult)
-    fill(T.wb[:, DUMP:DUMP + W], -1.0 / 32, ["wb"])
-    ts(T.wc[:, 5:6], T.wc[:, 1:2], T.wc[:, 2:3], A.add, ["wc1", "wc2"], ["wc5"])
-    ts(T.wc[:, 6:7], T.wc[:, 1:2], T.wc[:, 3:4], A.add, ["wc1", "wc3", "wc4"], ["wc6"], T.wc[:, 4:5], A.add)
-    ts(T.zka[:], T.row[:], grp, A.is_equal, ["row", "pf", "wc5"], ["zka"], T.wc[:, 5:6], A.mult)
-    ts(T.zkb[:], T.row[:], grp, A.is_equal, ["row", "pf", "wc6"], ["zkb"], T.wc[:, 6:7], A.mult)
-
-    came = {"a": ["l1a"], "b": ["l1b", "l1o"]}
     ca, cb = slice(a0 // 16, a0 // 16 + 40), slice(b0 // 16, b0 // 16 + 40)
-    pka, pkb = T.pp[:, 0:40], T.pp[:, 984:1024]
+    rb = slice(b0 // CAP, b0 // CAP + 4)
+    to_list(T.pp[:, 0:40], T.zk, T.w1, b0, b0 + H, True, True, ["zk", "w1b"], ["pp0"])
+    to_list(T.pt[:, cb], T.z0, T.w1, b0, b0 + H, True, True, ["z0", "w1b"], ["pt"])
 
-    def pads(h):
-        a, m, b = at[h], at[h] + H // 2, at[h] + H
-        act(T.nb2[:, a:m], T.pd[:].indirect(T.key2[:, a // 16:m // 16]), ["pd", "key2" + h], ["nb0" + h], -1.0)
-        ts(T.nb2[:, m:b], T.pd[:].indirect(T.key2[:, m // 16:b // 16]), -1.0, A.mult, ["pd", "key2" + h], ["nb1" + h])
+    def narrow(x):
+        r = pair[x] // CAP
+        ts(T.su[:, r:r + 2, 20:SEG], part(T.w1, x), -1.0, A.mult, ["w1b"], ["su%d" % x], 255.0, A.add)
 
-    def px(h, i):
-        return T["px" + h][:, 512 * i:512 * i + H // 2]
+    def keys(ps, c, rd, between):
+        ts(T.xk[:, c], ps, float(255 + 1024 * 255), A.add, rd, ["xk"])
+        between[0]()
+        ts(T.klo[:, c], T.xk[:, c], 255, A.bitwise_and, ["xk"], ["klo"])
+        ts(T.khi[:, c], T.xk[:, c], 2, A.arith_shift_right, ["xk"], ["khi"], P - 256, A.bitwise_and)
+        between[1]()
+        tt(T.k32[:, c], T.klo[:, c], T.khi[:, c], A.add, ["klo", "khi"], ["k32"])
 
-    def part(buf, h, i):
-        return buf[:, at[h] + i * H // 2:at[h] + (i + 1) * H // 2]
+    keys(T.pp[:, 0:40], cb, ["pp0"], [lambda: narrow(4), lambda: narrow(6)])
+    ts(T.su[:, rb, 10:20], T.pt[:, cb], 1536.0, A.add, ["pt"], ["sus"])
+    cp(T.su[:, rb, 0:10], T.k32[:, cb], ["k32"], ["suk"])
+    send(T.su, T.lu, (4, 5, 6, 7), "b1", ["su4", "su6", "suk", "sus"], None)
+    merge1(T.l1, me * CAP, CAP, "l1o")
+    fill(T.vl[:, ca], 1536.0, ["vla"])
 
-    def minus(h, src, start, stop, rd, which=(0, 1)):
-        for i in which:
-            mm(px(h, i), T.nid[:], part(src, h, i), start, stop, ["nid"] + rd, ["px%s%d" % (h, i)])
+    came = {0: ["l10", "l1o"], 2: ["l12"], 4: ["l1b"], 6: ["l1b"]}
 
-    def dests(h):
-        to_list(T["pt" + h][:, 0:40], T.z0, T.nb2, at[h], at[h] + H, h == "b", True, ["z0", "nb0" + h, "nb1" + h], ["pt" + h])
-        minus(h, T.nb2, False, True, ["nb0" + h, "nb1" + h])
+    def whole(x):
+        minus(x // 2, x, T.nq, False, True, ["nq%d" % x])
+        act(part(T.va, x, a0), bank[x // 2], ["bank%d" % (x // 2)], ["va%d" % x], 32.0, 32.0 * BIG)
 
-    to_list(pka, T.zka, T.l1, a0, a0 + H, True, True, ["zka", "l1a"], ["pp0"])
-    to_list(T.pta[:, 0:40], T.z0, T.l1, a0, a0 + H, True, False, ["z0", "l1a"], ["pta"])
-    minus("a", T.l1, True, False, came["a"])
-    ts(T.xk[:, ca], pka, float(256 + 512 * 256), A.add, ["pp0"], ["xka"])
-    ts(T.klo[:], T.xk[:, ca], 255, A.bitwise_and, ["xka"], ["klo"])
-    ts(T.khi[:], T.xk[:, ca], 1, A.arith_shift_right, ["xka"], ["khi"], P - 256, A.bitwise_and)
-    tt(T.k32[:, ca], T.klo[:], T.khi[:], A.add, ["klo", "khi"], ["k32a"])
-    cp(T.key2[:, ca], T.k32[:, ca], ["k32a"], ["key2a"])
-    pads("a")
-    to_list(pkb, T.zkb, T.l1, b0, b0 + H, True, True, ["zkb"] + came["b"], ["pp1"])
-    cp(T.xk[:, cb], pkb, ["pp1"], ["xkb"])
-    ts(T.k32[:, cb], T.xk[:, cb], P - 1, A.bitwise_and, ["xkb"], ["k32b"])
-    cp(T.key2[:, cb], T.k32[:, cb], ["k32b"], ["key2b"])
-    pads("b")
-    dests("a")
-    minus("b", T.l1, True, False, came["b"])
-    dests("b")
-    ts(T.v0[:], T.xk[:, cb], 16, A.arith_shift_right, ["xkb"], ["v0"])
-    ts(T.x2[:, ca], T.pta[:, 0:40], 1536.0, A.add, ["pta"], ["x2a"])
-    ts(T.vl[:], T.v0[:], 1536.0, A.add, ["v0"], ["vl"])
-    ts(part(T.nq, "a", 0), px("a", 0), 127.5 - BIG, A.add, ["pxa0"], ["nqa0"])
-    act(part(T.nq, "a", 1), px("a", 1), ["pxa1"], ["nqa1"], 1.0, 127.5 - BIG)
-    for i in range(2):
-        act(T.vb[:, i * H // 2:(i + 1) * H // 2], px("b", i), ["pxb%d" % i], ["vb%d" % i], 1.0 / 32, -1.0 / 32)
-    for i in range(2):
-        minus("a", T.l1, True, False, came["a"], (i,))
-        minus("a", T.nb2, False, False, ["nb0a", "nb1a"], (i,))
-        minus("a", T.nq, False, True, ["nqa%d" % i], (i,))
-        act(T.va[:, i * H // 2:(i + 1) * H // 2], px("a", i), ["pxa%d" % i], ["va%d" % i], -32.0, 32.0 * (BIG + 1))
-    tt(T.x2[:, cb], T.ptb[:, 0:40], T.vl[:], A.add, ["ptb", "vl"], ["x2b"])
-    ts(T.d2[:], T.x2[:], 1024 + N - 1, A.bitwise_and, ["x2a", "x2b"], ["d2"])
-    places("2", 80, lambda d: float(1024 + d), 1,
-           lambda: ts(T.tb[:], T.vb[:], 0.0, A.is_ge, ["vb0", "vb1"], ["tb"], -8.0, A.mult))
-    op("a", lambda e: e.activation(T.wa[:].indirect(T.o2[:, ca]), T.va[:], ACT.Silu), ["o2", "va0", "va1"], ["wa"])
-    tt(T.wb[:].indirect(T.o2[:, cb]), T.vb[:], T.tb[:], A.add, ["o2", "vb0", "vb1", "tb"], ["wb"])
+    def late(x):
+        minus(x // 2, x, T.nb2, True, False, ["nb%d" % x, "nb%d" % (x + 1)])
+        minus(x // 2, x, T.l1, False, False, came[x])
+        minus(x // 2, x, T.t1, False, True, ["t1"])
+        act(part(T.vb, x, b0), bank[x // 2], ["bank%d" % (x // 2)], ["vb%d" % x], -1.0 / 32, -(BIG + 256) / 32)
 
-    for c0, n, xs, sem in ((q2, 320, (2, 3), "b2"), (a0, H, (4, 5, 6, 7), "a2"), (q0, 320, (1,), "c2")):
+    def wrap(x):
+        ts(part(T.tb, x, b0), part(T.vb, x, b0), 0.0, A.is_ge, ["vb%d" % x], ["tb%d" % x], -8.0, A.mult)
+
+    def pads(x, sem):
+        q = me ^ x
+        out, got = T.nb2[:, q * CAP:(q + 1) * CAP], T.pd[:].indirect(T.lu[:, q, 0:10])
+        if x % 2 == 0:
+            act(out, got, ["pd", sem], ["nb%d" % x])
+        else:
+            cp(out, got, ["pd", sem], ["nb%d" % x])
+
+    pk = {0: (T.pp[:, 1004:1024], "pp1"), 2: (T.pp[:, 0:20], "pp0")}
+
+    def first_lists(x):
+        to_list(pk[x][0], T.zk, T.l1, pair[x], pair[x] + 320, True, True, ["zk"] + came[x], [pk[x][1]])
+
+    def own_pads(x):
+        c, k = slice(pair[x] // 16, pair[x] // 16 + 20), 10 * x
+        keys(pk[x][0], c, [pk[x][1]], [lambda: None] * 2)
+        cp(T.key2[:, k:k + 20], T.k32[:, c], ["k32"], ["key%d" % x])
+        act(T.nb2[:, pair[x]:pair[x] + CAP], T.pd[:].indirect(T.key2[:, k:k + 10]), ["pd", "key%d" % x], ["nb%d" % x])
+        cp(T.nb2[:, pair[x] + CAP:pair[x] + 320], T.pd[:].indirect(T.key2[:, k + 10:k + 20]),
+           ["pd", "key%d" % x], ["nb%d" % (x + 1)])
+
+    def both(x, src, start, rd):
+        for i in (2 + x // 2, x // 2):
+            minus(i, x, src, start, not start and i >= 2, rd)
+
+    first_lists(0)
+    both(0, T.l1, True, came[0])
+    own_pads(0)
+    first_lists(2)
+    both(0, T.nb2, False, ["nb0", "nb1"])
+    to_list(T.pt[:, ca], T.z0, T.l1, a0, a0 + H, True, False, ["z0"] + came[0] + came[2], ["pt"])
+    both(2, T.l1, True, came[2])
+    act(part(T.nq, 0), bank[2], ["bank2"], ["nq0"], 1.0, BIG - 128.5)
+    own_pads(2)
+    to_list(T.pt[:, ca], T.z0, T.nb2, a0, a0 + H, False, True, ["z0", "nb0", "nb1", "nb2", "nb3"], ["pt"])
+    minus(3, 2, T.nb2, False, True, ["nb2", "nb3"])
+    for x in (4, 5, 6, 7):
+        pads(x, "lub")
+    to_list(T.pt[:, cb], T.z0, T.nb2, b0, b0 + H, True, True, ["z0", "nb4", "nb5", "nb6", "nb7"], ["pt"])
+    minus(1, 2, T.nb2, False, False, ["nb2", "nb3"])
+    act(part(T.nq, 2), bank[3], ["bank3"], ["nq2"], 1.0, BIG - 128.5)
+    cp(T.vl[:, cb], T.lu[:, rb, 10:20], ["lub"], ["vlb"])
+    ts(T.l1[:, b0:b0 + H], T.lu[:, rb, 20:SEG], -1.0, A.mult, ["lub"], ["l1b"], 255.0, A.add)
+    ts(T.t1[:, b0:b0 + H], T.lu[:, rb, 20:SEG], BIG - 127.5, A.add, ["lub"], ["t1"])
+    tt(T.x2[:], T.pt[:, 0:80], T.vl[:], A.add, ["pt", "vla", "vlb"], ["x2"])
+    marks("2", 0, 80, 1024 + N - 1, lambda d: float(1024 + N - 1 - d), "2")
+    late(4)
+    late(6)
+    whole(0)
+    whole(2)
+    places("2", 80, "2", 1, [lambda: None, lambda: wrap(4), lambda: wrap(6), lambda: None])
+    op("a", lambda e: e.activation(T.wa[:].indirect(T.o2[:, ca]), T.va[:], ACT.Silu), ["o2_%d" % (a0 // H), "va0", "va2"], ["wa"])
+    tt(T.wb[:].indirect(T.o2[:, cb]), T.vb[:], T.tb[:], A.add, ["o2_%d" % (b0 // H), "vb4", "vb6", "tb4", "tb6"], ["wb"])
+
+    q1 = (me ^ 1) * CAP
+    for c0, n, xs, sem in ((q1, CAP, (1,), "m2"), (b0, H, (4, 5, 6, 7), "b2"), (pair[2], 320, (2, 3), "a2"), (me * CAP, CAP, (), "o")):
         scan(T.w2[:, c0:c0 + n], T.wa[:, DUMP + c0:DUMP + c0 + n], T.wb[:, DUMP + c0:DUMP + c0 + n], -1.0, A.max, A.mult,
              ["wa", "wb"], ["w2" + sem])
-        send(T.w2, T.l2, xs, sem, ["w2" + sem])
+        if xs:
+            send(T.w2, T.l2, xs, sem, ["w2" + sem])
 
     def widen(q, src, a, b, rd, wr):
         if q == "a":
@@ -336,15 +417,15 @@ def rank_program(g, core, T, topo):
     def store(q, a, b, rd, sem):
         op(q, lambda e: e.dma_start(T.y[:, a:b], T.yy[:, a:b]), rd, [], sem)
 
-    widen("a", T.w2, me * CAP, (me + 1) * CAP, ["w2c2"], ["yo"])
-    widen("a", T.l2, q2, q2 + 320, ["l2b"], ["yb"])
-    store("a", q2, q2 + 320, ["yb"], "st_b")
-    widen("v", T.l2, a0, a0 + 320, ["l2a"], ["ya0"])
-    widen("a", T.l2, a0 + 320, a0 + H, ["l2a"], ["ya1"])
-    store("s", a0, a0 + H, ["ya0", "ya1"], "st_a")
-    q1 = (me ^ 1) * CAP
-    widen("v", T.l2, q1, q1 + CAP, ["l2c"], ["yc"])
-    store("a", q0, q0 + 320, ["yc", "yo"], "st_c")
+    widen("a", T.w2, me * CAP, (me + 1) * CAP, ["w2o"], ["yo"])
+    widen("v", T.l2, q1, q1 + CAP, ["l2m"], ["ym"])
+    store("s", pair[0], pair[0] + 320, ["ym", "yo"], "st_c")
+    widen("v", T.l2, b0, b0 + 384, ["l2b"], ["yb0"])
+    widen("a", T.l2, b0 + 384, b0 + H, ["l2b"], ["yb1"])
+    store("s", b0, b0 + H, ["yb0", "yb1"], "st_b")
+    widen("v", T.l2, pair[2], pair[2] + 224, ["l2a"], ["ya0"])
+    widen("a", T.l2, pair[2] + 224, pair[2] + 320, ["l2a"], ["ya1"])
+    store("s", pair[2], pair[2] + 320, ["ya0", "ya1"], "st_a")
 
     emit(g, T, ops, landed)
     for s in ("st_a", "st_b", "st_c"):

from concourse.bass import DstId, RemoteDMATransfer
from concourse.mybir import AluOpType, ActivationFunctionType

N, C, CAP, P = 8, 1024, 160, 8192
W = N * CAP
H = W // 2
DUMP = 1408
LIFT = 2048 + DUMP
NS = 416
FILL = 2.0 ** 20
SEG = 20 + CAP
BIG = 49152

BF, F16, F32, I32, U16 = "bfloat16", "float16", "float32", "int32", "uint16"


def _sb(n, t):
    return ("sbuf", [128, n], t)


def _ps(n):
    return ("psum", [128, n], F32)


SCRATCH = {
    "fst": _sb(64, I32), "p0": _sb(512, BF), "cv": _sb(C, BF), "pd": _sb(P, BF),
    "pi": _sb(8, I32), "pf": _sb(8, F32), "wc": _sb(8, F32), "row": _sb(144, F32), "blk": _sb(128, BF),
    "onehot": _sb(16, BF), "za": _sb(144, BF), "z0": _sb(144, BF), "zk": _sb(144, BF),
    "nob": _sb(128, BF), "m1a": _sb(128, BF), "m1": _sb(128, BF), "nid": _sb(128, BF),
    "dd": _sb(640, F32), "ones": _sb(144, BF), "z8": _sb(144, BF), "c0": _sb(C, BF),
    "hi32": _sb(64, I32), "lo32": _sb(64, I32), "hi16": _sb(64, U16), "lo16": _sb(64, U16), "key1": _sb(64, U16),
    "msk": _sb(C, BF), "gm": _sb(C, BF),
    "x1": _sb(80, I32), "d1": _sb(80, I32), "e1": _sb(640, BF), "s1": _sb(640, BF), "f1": _sb(640, F32), "o1": _sb(80, U16),
    "x2": _sb(80, I32), "d2": _sb(80, I32), "e2": _sb(640, BF), "s2": _sb(640, BF), "f2": _sb(640, F32), "o2": _sb(80, U16),
    "nb1": _sb(C, BF), "cs": _sb(C, BF), "va1": _sb(NS, F32), "ws1": _sb(W, F32), "wd1": _sb(W, BF), "w1": _sb(W, F16), "l1": _sb(W, F16),
    "xk": _sb(80, I32), "klo": _sb(80, I32), "khi": _sb(80, I32), "k32": _sb(80, I32), "key2": _sb(40, U16),
    "su": ("sbuf", [128, N, SEG], U16), "lu": ("sbuf", [128, N, SEG], U16),
    "vl": _sb(80, F32), "t1": _sb(W, BF),
    "nb2": _sb(W, BF), "nq": _sb(W, BF), "va": _sb(H, F32), "vb": _sb(H, BF), "tb": _sb(H, BF),
    "wa": _sb(DUMP + W, F32), "wb": _sb(DUMP + W, BF), "w2": _sb(W, BF), "l2": _sb(W, BF), "yy": _sb(W, F32),
    "pp": _ps(1024), "pt": _ps(512), "pxa": _ps(1024), "pxb": _ps(1024),
}
SEMAPHORES = ["cv_", "ca_", "cp_", "cg_", "ld_f", "ld_0", "ld_1", "ld_c", "ld_p", "st_a", "st_b", "st_c",
              "m1", "a1", "b1", "m2", "a2", "b2", "sent"]

A = AluOpType
ACT = ActivationFunctionType


def emit(g, T, ops, landed):
    eng = {"v": g.vector, "a": g.scalar, "p": g.tensor, "g": g, "s": g.sync}
    cnt = {"v": "cv_", "a": "ca_", "p": "cp_", "g": "cg_"}
    writer = {t: ("x",) + e for t, e in landed.items()}
    readers = {}
    known = {q: {} for q in eng}
    after = []
    waits = []
    signal = set()
    for i, (q, call, rd, wr, dma) in enumerate(ops):
        need = []
        for t in rd:
            if t in writer:
                need.append(writer[t])
        for t in wr:
            if t in writer:
                need.append(writer[t])
            need.extend(readers.get(t, []))
        need.sort(key=lambda e: -e[1] if e[0] == "o" else 1)
        mine = []
        for e in need:
            if e[0] == "x":
                key, val, more = e[1], e[2], {}
            else:
                j = e[1]
                if ops[j][0] == "p" and q == "p":
                    continue
                key, val, more = (ops[j][4], 16, after[j]) if ops[j][4] else (ops[j][0], j, after[j])
            if known[q].get(key, -1) >= val:
                continue
            mine.append(e)
            known[q][key] = val
            for k, v in more.items():
                if known[q].get(k, -1) < v:
                    known[q][k] = v
            if e[0] == "o" and not ops[e[1]][4]:
                signal.add(e[1])
        waits.append(mine)
        after.append(dict(known[q]))
        for t in rd:
            readers.setdefault(t, []).append(("o", i))
        for t in wr:
            writer[t] = ("o", i)
            readers[t] = []
    n = {q: 0 for q in cnt}
    value = {}
    for i, (q, call, rd, wr, dma) in enumerate(ops):
        for e in waits[i]:
            if e[0] == "x":
                eng[q].wait_ge(T.sem[e[1]], e[2])
            elif ops[e[1]][4]:
                eng[q].wait_ge(T.sem[ops[e[1]][4]], 16)
            else:
                eng[q].wait_ge(T.sem[cnt[ops[e[1]][0]]], value[e[1]])
        ins = call(eng[q])
        if dma:
            ins.then_inc(T.sem[dma], 16)
        elif i in signal:
            n[q] += 1
            value[i] = n[q]
            ins.then_inc(T.sem[cnt[q]], 1)


def rank_program(g, core, T, topo):
    me = T.rank_of(core)
    if me is None:
        return
    ops = []

    def op(q, call, rd, wr, dma=None):
        ops.append((q, call, list(rd), list(wr), dma))

    def ts(out, in0, s1, o0, rd, wr, s2=None, o1=None):
        if o1 is None:
            op("v", lambda e: e.tensor_scalar(out, in0, s1, None, o0), rd, wr)
        else:
            op("v", lambda e: e.tensor_scalar(out, in0, s1, s2, o0, o1), rd, wr)

    def tt(out, in0, in1, o, rd, wr):
        op("v", lambda e: e.tensor_tensor(out, in0, in1, o), rd, wr)

    def cp(out, in_, rd, wr):
        op("v", lambda e: e.tensor_copy(out, in_), rd, wr)

    def scan(out, d0, d1, first, o0, o1, rd, wr):
        op("v", lambda e: e.tensor_tensor_scan(out, d0, d1, first, o0, o1), rd, wr)

    def fill(out, val, wr):
        op("v", lambda e: e.memset(out, val), [], wr)

    def act(out, in_, rd, wr, scale=1.0, bias=0.0, func=ACT.Identity):
        op("a", lambda e: e.activation(out, in_, func, bias=bias, scale=scale), rd, wr)

    def mm(out, lhs, rhs, start, stop, rd, wr):
        op("p", lambda e: e.matmul(out, lhs, rhs, start, stop), rd, wr)

    def iota(out, pattern, base, cm, wr, small=True):
        if small:
            op("g", lambda e: e.iota(out, pattern, base, cm, allow_small_or_imprecise_dtypes=True), [], wr)
        else:
            op("g", lambda e: e.iota(out, pattern, base, cm), [], wr)

    def sel(out, in_, cmp_op, val, rd, wr):
        op("g", lambda e: e.affine_select(out, in_, [[-1, 128]], cmp_op, val, 0, 1), rd, wr)

    def to_list(out, z, src, c0, c1, start, stop, rd, wr):
        for r in range(16):
            mm(out, z[:, 15 - r:143 - r], src[:, c0 + r:c1:16], start and r == 0, stop and r == 15, rd, wr)

    def marks(h, a, b, mask, match, tag, between=lambda: None):
        ts(T["d" + h][:, a:b], T["x" + h][:, a:b], mask, A.bitwise_and, ["x" + tag], ["d" + tag])
        between()
        for d in range(N):
            ts(T["e" + h][:, 8 * a + d:8 * b:8], T["d" + h][:, a:b], match(d), A.is_equal, ["d" + tag], ["e%s_%d" % (tag, d)])

    def places(h, n, last, less, between):
        ee, ss, ff, oo = T["e" + h], T["s" + h], T["f" + h], T["o" + h]
        et = ["e%s_%d" % (last, d) for d in range(N)]
        st = ["s%s_%d" % (h, d) for d in range(N)]
        k = 4 * n
        for b in range(2):
            mm(T.pp[:, 512 - k + b * k:512 + b * k], T.m1[:], ee[:, b * k:b * k + k], True, False, et + ["m1"], ["pp%d" % b])
        for d in range(N):
            scan(ss[:, d:8 * n:8], T.ones[:, 0:n], ee[:, d:8 * n:8], float(128 - 10 * d), A.mult, A.subtract,
                 et[0:4 + d // 4 * 4] + ["ones"], [st[d]])
        for b in range(2):
            between[b]()
            mm(T.pp[:, 512 - k + b * k:512 + b * k], T.nob[:], ss[:, b * k:b * k + k], False, True, st + ["nob"], ["pp%d" % b])
        between[2]()
        for b in range(2):
            scan(ff[:, b * k:b * k + k], T.dd[:, b * k:b * k + k], T.pp[:, 512 - k + b * k:512 + b * k], 8192.0,
                 A.min, A.max, ["dd", "pp%d" % b], ["f%s_%d" % (h, b)])
        for b in range(2):
            ts(oo[:, b * n // 2:(b + 1) * n // 2], ff[:, b * k + 7:b * k + k:8], float(-less), A.add,
               ["f%s_%d" % (h, b)], ["o%s_%d" % (h, b)])
            if b == 0:
                between[3]()

    sent = [0]

    def send(win, land, xs, sem, rd, seg=CAP):
        tr = []
        for i, x in enumerate(xs):
            q = me ^ x
            dst = T.cores[q]
            engines = topo.engines(core, dst)
            k = len(engines) // len(xs)
            mask = sum(1 << e for e in engines[i * k:(i + 1) * k])
            rid, pid = topo.addr(dst)[0:2]
            if seg:
                tr.append((win[:, q * seg:(q + 1) * seg], land[:, me * seg:(me + 1) * seg], rid, pid, mask))
            else:
                tr.append((win[:, q, :], land[:, me, :], rid, pid, mask))
            sent[0] += k
        op("g", lambda e: e.remote_dma_fused(
            [RemoteDMATransfer(dst_ids=[DstId(rid=t[2], pnc=t[3])], dma_engine_mask=t[4], remote_sem=T.sem[sem],
                               src=t[0], dst=t[1]) for t in tr], local_sem=T.sem.sent), rd, [])

    per = len(topo.engines(core, T.cores[me ^ 1]))
    landed = {"l10": ("m1", per), "l12": ("a1", per), "lub": ("b1", per), "l2m": ("m2", per), "l2a": ("a2", per), "l2b": ("b2", per)}

    op("s", lambda e: e.dma_start(T.fst[:], T.first[:]), [], ["fst"], "ld_f")
    op("s", lambda e: e.dma_start(T.p0[:], T.pads[0:128:16, :]), [], ["p0"], "ld_0")
    op("s", lambda e: e.dma_start(T.c0[0:8, :], T.cells[0:128:16, :]), [], ["c0"], "ld_1")
    op("s", lambda e: e.dma_start(T.pd[:], T.pads[:]), [], ["pd"], "ld_p")
    op("s", lambda e: e.dma_start(T.cv[:], T.cells[:]), [], ["cv"], "ld_c")

    fill(T.ones[:], 1.0, ["ones"])
    act(T.ws1[:, 0:144], T.ones[:], ["ones"], ["ws1a"], FILL, 0.0, ACT.Silu)
    fill(T.wd1[:], -1.0 / 1024, ["wd1"])
    iota(T.pi[:, 2:3], [[0, 1]], 0, 1, ["pi2"], small=False)
    iota(T.row[:], [[1, 144]], -15, 0, ["row"])
    iota(T.blk[:], [[16, 8], [0, 16]], 0, 0, ["blk"])
    ts(T.pi[:, 0:1], T.pi[:, 2:3], 112, A.bitwise_and, ["pi2"], ["pi0"])
    ts(T.pi[:, 1:2], T.pi[:, 2:3], 15, A.bitwise_and, ["pi2"], ["pi1"])
    cp(T.pf[:, 0:2], T.pi[:, 0:2], ["pi0", "pi1"], ["pf"])
    grp, sym = T.pf[:, 0:1], T.pf[:, 1:2]
    ts(T.wc[:, 0:1], sym, 0.0, A.is_equal, ["pf"], ["wc0"])
    ts(T.onehot[:], T.row[:, 15:31], sym, A.is_equal, ["row", "pf"], ["onehot"])
    ts(T.za[:], T.row[:], grp, A.is_equal, ["row", "pf"], ["za"], -1.0, A.mult)
    ts(T.z0[:], T.row[:], grp, A.is_equal, ["row", "pf", "wc0"], ["z0"], T.wc[:, 0:1], A.mult)
    ts(T.nob[:], T.blk[:], grp, A.is_equal, ["blk", "pf"], ["nob"], -1.0, A.mult)
    op("g", lambda e: e.affine_select(T.z8[0:8, :], T.ones[0:8, :], [[1, 144]], A.is_equal, 0.0, -15, -16), ["ones"], ["z8"])
    sel(T.nid[:], T.nob[:], A.is_equal, 0.0, ["nob"], ["nid"])
    sel(T.m1a[:], T.nob[:], A.is_gt, 0.0, ["nob"], ["m1a"])
    sel(T.m1[:], T.m1a[:], A.not_equal, float(LIFT), ["m1a"], ["m1"])
    iota(T.dd[:], [[-16, 80], [8192, 8]], DUMP - 16, -1, ["dd"])
    iota(T.ws1[:, 144:W], [[0, W - 144]], int(FILL), 0, ["ws1b"])

    ts(T.hi32[:], T.fst[:], 9, A.logical_shift_right, ["fst"], ["hi32"])
    ts(T.lo32[:], T.fst[:], 511, A.bitwise_and, ["fst"], ["lo32"])
    cp(T.hi16[:], T.hi32[:], ["hi32"], ["hi16"])
    cp(T.lo16[:], T.lo32[:], ["lo32"], ["lo16"])
    for r in range(16):
        mm(T.pt[:, 0:64], T.z8[0:8, 15 - r:143 - r], T.c0[0:8, r:C:16], r == 0, False, ["z8", "c0"], ["pt"])
    parts = ((0, 192), (192, 576), (576, C))
    for i, (a, b) in enumerate(parts):
        hot = T.onehot[:].indirect(T.hi16[:, a // 16:b // 16])
        (cp if i == 0 else act)(T.msk[:, a:b], hot, ["onehot", "hi16"], ["msk%d" % i])
        if i == 0:
            cp(T.key1[:], T.fst[:], ["fst"], ["key1"])
    for i, (a, b) in enumerate(parts):
        tt(T.gm[:, a:b], T.p0[:].indirect(T.lo16[:, a // 16:b // 16]), T.msk[:, a:b], A.mult,
           ["p0", "lo16", "msk%d" % i], ["gm%d" % i])
    to_list(T.pt[:, 0:64], T.za, T.gm, 0, C, False, True, ["za", "gm0", "gm1", "gm2"], ["pt"])
    act(T.wb[:, DUMP:DUMP + W], T.wd1[:], ["wd1"], ["wb"], 32.0)
    na = C - NS
    mid = na // 64 * 32
    px1 = T.pxb[:, 0:NS]
    for i, wgt in enumerate((-1.0, -1024.0)):
        ts(T.wc[:, 1 + i:2 + i], sym, float(1 + i), A.is_equal, ["pf"], ["wc%d" % (1 + i)], wgt, A.mult)
    ts(T.wc[:, 3:4], T.wc[:, 1:2], T.wc[:, 2:3], A.add, ["wc1", "wc2"], ["wc3"])
    ts(T.zk[:], T.row[:], grp, A.is_equal, ["row", "pf", "wc3"], ["zk"], T.wc[:, 3:4], A.mult)

    def scaled(i, a, b):
        ts(T.cs[:, a:b], T.cv[:, a:b], 1.0, A.add, ["cv"], ["cs%d" % i], -1.0 / FILL, A.mult)

    def pads1(a, b, scale, tag):
        act(T.nb1[:, a:b], T.pd[:].indirect(T.key1[:, a // 16:b // 16]), ["pd", "key1"], [tag], scale)

    pads1(na, C, -1.0, "nb1s")
    pads1(0, mid, 1.0 / FILL, "nb10")
    ts(T.x1[:, 0:64], T.pt[:, 0:64], 256.0, A.add, ["pt"], ["x1"])
    marks("1", 0, 64, N - 1, lambda d: float(d), "1")

    def reduce1():
        mm(px1, T.nid[:], T.nb1[:, na:C], True, False, ["nid", "nb1s"], ["bank2"])
        mm(px1, T.nid[:], T.cv[:, na:C], False, True, ["nid", "cv"], ["bank2"])
        pads1(mid, na, 1.0 / FILL, "nb11")
        act(T.va1[:], px1, ["bank2"], ["va1"], -1024.0, 1024.0 * 257)

    places("1", 64, "1", DUMP + 1, [lambda: None, lambda: None, reduce1, lambda: scaled(0, 0, mid)])
    op("a", lambda e: e.activation(T.ws1[:].indirect(T.o1[:, na // 16:C // 16]), T.va1[:], ACT.Silu),
       ["o1_1", "va1"], ["ws1a", "ws1b"])
    for i, (a, b) in enumerate(((0, mid), (mid, na))):
        if i:
            scaled(i, a, b)
        tt(T.wd1[:].indirect(T.o1[:, a // 16:b // 16]), T.cs[:, a:b], T.nb1[:, a:b], A.add,
           ["o1_0", "o1_%d" % i, "cs%d" % i, "nb1%d" % i], ["wd1"])
    a0 = H * (me // 4)
    b0 = H - a0
    pair = {x: ((me ^ x) // 2) * 2 * CAP for x in (0, 2, 4, 6)}

    def merge1(out, a, n, tag):
        scan(out[:, a:a + n], T.ws1[:, a:a + n], T.wd1[:, a:a + n], -1.0, A.max, A.mult, ["ws1a", "ws1b", "wd1"], [tag])

    merge1(T.w1, (me ^ 1) * CAP, CAP, "w11")
    send(T.w1, T.l1, (1,), "m1", ["w11"])
    bank = [T.pxa[:, 0:320], T.pxa[:, 512:832], T.pxb[:, 0:320], T.pxb[:, 512:832]]

    def part(buf, x, off=0):
        return buf[:, pair[x] - off:pair[x] - off + 320]

    def minus(i, x, src, start, stop, rd):
        mm(bank[i], T.nid[:], part(src, x), start, stop, ["nid"] + rd, ["bank%d" % i])

    merge1(T.w1, b0, H, "w1b")
    merge1(T.w1, pair[2], 320, "w12")
    send(T.w1, T.l1, (2, 3), "a1", ["w12"])
    act(T.wa[:, DUMP:DUMP + W], T.pd[:, 0:W], ["pd"], ["wa"], 0.0, 32.0, ACT.Silu)

    ca, cb = slice(a0 // 16, a0 // 16 + 40), slice(b0 // 16, b0 // 16 + 40)
    rb = slice(b0 // CAP, b0 // CAP + 4)
    to_list(T.pp[:, 0:40], T.zk, T.w1, b0, b0 + H, True, True, ["zk", "w1b"], ["pp0"])
    to_list(T.pt[:, cb], T.z0, T.w1, b0, b0 + H, True, True, ["z0", "w1b"], ["pt"])

    def narrow(x):
        r = pair[x] // CAP
        ts(T.su[:, r:r + 2, 20:SEG], part(T.w1, x), -1.0, A.mult, ["w1b"], ["su%d" % x], 255.0, A.add)

    def keys(ps, c, rd, between):
        ts(T.xk[:, c], ps, float(255 + 1024 * 255), A.add, rd, ["xk"])
        between[0]()
        ts(T.klo[:, c], T.xk[:, c], 255, A.bitwise_and, ["xk"], ["klo"])
        ts(T.khi[:, c], T.xk[:, c], 2, A.arith_shift_right, ["xk"], ["khi"], P - 256, A.bitwise_and)
        between[1]()
        tt(T.k32[:, c], T.klo[:, c], T.khi[:, c], A.add, ["klo", "khi"], ["k32"])

    keys(T.pp[:, 0:40], cb, ["pp0"], [lambda: narrow(4), lambda: narrow(6)])
    ts(T.su[:, rb, 10:20], T.pt[:, cb], 1536.0, A.add, ["pt"], ["sus"])
    cp(T.su[:, rb, 0:10], T.k32[:, cb], ["k32"], ["suk"])
    send(T.su, T.lu, (4, 5, 6, 7), "b1", ["su4", "su6", "suk", "sus"], None)
    merge1(T.l1, me * CAP, CAP, "l1o")
    fill(T.vl[:, ca], 1536.0, ["vla"])

    came = {0: ["l10", "l1o"], 2: ["l12"], 4: ["l1b"], 6: ["l1b"]}

    def whole(x):
        minus(x // 2, x, T.nq, False, True, ["nq%d" % x])
        act(part(T.va, x, a0), bank[x // 2], ["bank%d" % (x // 2)], ["va%d" % x], 32.0, 32.0 * BIG)

    def late(x):
        minus(x // 2, x, T.nb2, True, False, ["nb%d" % x, "nb%d" % (x + 1)])
        minus(x // 2, x, T.l1, False, False, came[x])
        minus(x // 2, x, T.t1, False, True, ["t1"])
        act(part(T.vb, x, b0), bank[x // 2], ["bank%d" % (x // 2)], ["vb%d" % x], -1.0 / 32, -(BIG + 256) / 32)

    def wrap(x):
        ts(part(T.tb, x, b0), part(T.vb, x, b0), 0.0, A.is_ge, ["vb%d" % x], ["tb%d" % x], -8.0, A.mult)

    def pads(x, sem):
        q = me ^ x
        out, got = T.nb2[:, q * CAP:(q + 1) * CAP], T.pd[:].indirect(T.lu[:, q, 0:10])
        if x % 2 == 0:
            act(out, got, ["pd", sem], ["nb%d" % x])
        else:
            cp(out, got, ["pd", sem], ["nb%d" % x])

    pk = {0: (T.pp[:, 1004:1024], "pp1"), 2: (T.pp[:, 0:20], "pp0")}

    def first_lists(x):
        to_list(pk[x][0], T.zk, T.l1, pair[x], pair[x] + 320, True, True, ["zk"] + came[x], [pk[x][1]])

    def own_pads(x):
        c, k = slice(pair[x] // 16, pair[x] // 16 + 20), 10 * x
        keys(pk[x][0], c, [pk[x][1]], [lambda: None] * 2)
        cp(T.key2[:, k:k + 20], T.k32[:, c], ["k32"], ["key%d" % x])
        act(T.nb2[:, pair[x]:pair[x] + CAP], T.pd[:].indirect(T.key2[:, k:k + 10]), ["pd", "key%d" % x], ["nb%d" % x])
        cp(T.nb2[:, pair[x] + CAP:pair[x] + 320], T.pd[:].indirect(T.key2[:, k + 10:k + 20]),
           ["pd", "key%d" % x], ["nb%d" % (x + 1)])

    def both(x, src, start, rd):
        for i in (2 + x // 2, x // 2):
            minus(i, x, src, start, not start and i >= 2, rd)

    first_lists(0)
    both(0, T.l1, True, came[0])
    own_pads(0)
    first_lists(2)
    both(0, T.nb2, False, ["nb0", "nb1"])
    to_list(T.pt[:, ca], T.z0, T.l1, a0, a0 + H, True, False, ["z0"] + came[0] + came[2], ["pt"])
    both(2, T.l1, True, came[2])
    act(part(T.nq, 0), bank[2], ["bank2"], ["nq0"], 1.0, BIG - 128.5)
    own_pads(2)
    to_list(T.pt[:, ca], T.z0, T.nb2, a0, a0 + H, False, True, ["z0", "nb0", "nb1", "nb2", "nb3"], ["pt"])
    minus(3, 2, T.nb2, False, True, ["nb2", "nb3"])
    for x in (4, 5, 6, 7):
        pads(x, "lub")
    to_list(T.pt[:, cb], T.z0, T.nb2, b0, b0 + H, True, True, ["z0", "nb4", "nb5", "nb6", "nb7"], ["pt"])
    minus(1, 2, T.nb2, False, False, ["nb2", "nb3"])
    act(part(T.nq, 2), bank[3], ["bank3"], ["nq2"], 1.0, BIG - 128.5)
    cp(T.vl[:, cb], T.lu[:, rb, 10:20], ["lub"], ["vlb"])
    ts(T.l1[:, b0:b0 + H], T.lu[:, rb, 20:SEG], -1.0, A.mult, ["lub"], ["l1b"], 255.0, A.add)
    ts(T.t1[:, b0:b0 + H], T.lu[:, rb, 20:SEG], BIG - 127.5, A.add, ["lub"], ["t1"])
    tt(T.x2[:], T.pt[:, 0:80], T.vl[:], A.add, ["pt", "vla", "vlb"], ["x2"])
    marks("2", 0, 80, 1024 + N - 1, lambda d: float(1024 + N - 1 - d), "2")
    late(4)
    late(6)
    whole(0)
    whole(2)
    places("2", 80, "2", 1, [lambda: None, lambda: wrap(4), lambda: wrap(6), lambda: None])
    op("a", lambda e: e.activation(T.wa[:].indirect(T.o2[:, ca]), T.va[:], ACT.Silu), ["o2_%d" % (a0 // H), "va0", "va2"], ["wa"])
    tt(T.wb[:].indirect(T.o2[:, cb]), T.vb[:], T.tb[:], A.add, ["o2_%d" % (b0 // H), "vb4", "vb6", "tb4", "tb6"], ["wb"])

    q1 = (me ^ 1) * CAP
    for c0, n, xs, sem in ((q1, CAP, (1,), "m2"), (b0, H, (4, 5, 6, 7), "b2"), (pair[2], 320, (2, 3), "a2"), (me * CAP, CAP, (), "o")):
        scan(T.w2[:, c0:c0 + n], T.wa[:, DUMP + c0:DUMP + c0 + n], T.wb[:, DUMP + c0:DUMP + c0 + n], -1.0, A.max, A.mult,
             ["wa", "wb"], ["w2" + sem])
        if xs:
            send(T.w2, T.l2, xs, sem, ["w2" + sem])

    def widen(q, src, a, b, rd, wr):
        if q == "a":
            act(T.yy[:, a:b], src[:, a:b], rd, wr, -1.0, -1.0)
        else:
            ts(T.yy[:, a:b], src[:, a:b], -1.0, A.mult, rd, wr, -1.0, A.add)

    def store(q, a, b, rd, sem):
        op(q, lambda e: e.dma_start(T.y[:, a:b], T.yy[:, a:b]), rd, [], sem)

    widen("a", T.w2, me * CAP, (me + 1) * CAP, ["w2o"], ["yo"])
    widen("v", T.l2, q1, q1 + CAP, ["l2m"], ["ym"])
    store("s", pair[0], pair[0] + 320, ["ym", "yo"], "st_c")
    widen("v", T.l2, b0, b0 + 384, ["l2b"], ["yb0"])
    widen("a", T.l2, b0 + 384, b0 + H, ["l2b"], ["yb1"])
    store("s", b0, b0 + H, ["yb0", "yb1"], "st_b")
    widen("v", T.l2, pair[2], pair[2] + 224, ["l2a"], ["ya0"])
    widen("a", T.l2, pair[2] + 224, pair[2] + 320, ["l2a"], ["ya1"])
    store("s", pair[2], pair[2] + 320, ["ya0", "ya1"], "st_a")

    emit(g, T, ops, landed)
    for s in ("st_a", "st_b", "st_c"):
        g.sync.wait_ge(T.sem[s], 16)
    g.wait_ge(T.sem.sent, sent[0])
